import numpy as np
import ml_dtypes


def mxq(x, axis, fmt="e4m3"):
    dtype, down = {"e4m3": (ml_dtypes.float8_e4m3fn, 7), "e5m2": (ml_dtypes.float8_e5m2, 14)}[fmt]
    v = np.moveaxis(np.asarray(x, np.float32).astype(ml_dtypes.bfloat16).astype(np.float64), axis, -1)
    blocks = v.reshape(v.shape[:-1] + (-1, 32))
    amax = np.abs(blocks).max(-1, keepdims=True)
    byte = np.maximum(np.where(amax > 0, np.frexp(amax)[1] - 1 + 127, 0) - down, 1)
    scale = np.exp2(byte - 127.0)
    codes = (blocks / scale).astype(np.float32).astype(dtype).astype(np.float64)
    return np.moveaxis((codes * scale).reshape(v.shape), -1, axis)


WIDE = False


def mx_kscale(k):
    if not WIDE:
        return np.ones(k)
    levels = np.array([10, -10, 5, -5, 0])
    if k % 512:
        return np.exp2(np.random.permutation(np.resize(levels, k // 32))).repeat(32)
    a = np.empty((k // 512, 16))
    for p in range(k // 512):
        a[p, :8] = np.random.permutation(np.resize(levels, 8))
        for g in range(8):
            far = levels[np.abs(levels - a[p, g]) >= 10]
            a[p, g + 8] = far[np.random.randint(len(far))]
    return np.exp2(a.ravel()).repeat(32)


def f64(x):
    return np.asarray(x).astype(np.float64)


def striped(idx):
    return np.tile(np.asarray(idx).reshape(-1, 16).T, (8, 1)).astype(np.uint16)


def unstriped(offs):
    return offs[:16].T.reshape(-1).astype(np.int64)


E2M1 = np.array([0.0, 0.5, 1.0, 1.5, 2.0, 3.0, 4.0, 6.0, -0.0, -0.5, -1.0, -1.5, -2.0, -3.0, -4.0, -6.0])


def pack_weight(w, fmt):
    k, n = w.shape
    w = f64(np.asarray(w, np.float32).astype(ml_dtypes.bfloat16)).reshape(k // 32, 32, n)
    amax = np.abs(w).max(1)
    if fmt == "e4m3":
        byte = np.frexp(amax)[1] - 1 + 127 - 7
    else:
        mant, ex = np.frexp(amax / 6.0)
        byte = np.where(mant > 0.5, ex, ex - 1) + 127
    byte = np.clip(np.where(amax > 0, byte, 1), 1, 254)
    scaled = (w * np.exp2(127.0 - byte)[:, None, :]).reshape(k, n).astype(np.float32)
    by_word = np.ascontiguousarray(scaled.reshape(k // 512, 128, 4, n).transpose(0, 1, 3, 2))
    if fmt == "e4m3":
        words = by_word.astype(ml_dtypes.float8_e4m3fn).view(np.uint8)
    else:
        c = by_word.astype(ml_dtypes.float4_e2m1fn).view(np.uint8) & 0xF
        words = (c[..., 0::2] | (c[..., 1::2] << 4)).reshape(k // 512, 128, 2 * n)
    return np.ascontiguousarray(words), np.ascontiguousarray(byte.astype(np.uint8).reshape(k // 512, 16, n))


def unpack_weight(words, scales, fmt):
    g, _, n = scales.shape
    words = np.ascontiguousarray(words).reshape(g, 128, n, -1)
    if fmt == "e4m3":
        vals = words.view(ml_dtypes.float8_e4m3fn).astype(np.float64)
    else:
        nib = np.empty((g, 128, n, 4), np.uint8)
        nib[..., 0::2] = words & 0xF
        nib[..., 1::2] = words >> 4
        vals = E2M1[nib]
    vals = vals * np.repeat(np.exp2(scales.astype(np.float64) - 127.0), 8, axis=1)[..., None]
    return vals.transpose(0, 1, 3, 2).reshape(g * 512, n)


def bf(x):
    return np.asarray(x, np.float32).astype(ml_dtypes.bfloat16)


def planes(Y):
    r, m = Y.shape
    b = f64(bf(Y)).reshape(r // 32, 32, m)
    amax = np.abs(b).max(1)
    byte = np.clip(np.where(amax > 0, np.frexp(amax)[1] - 1 + 127 - 7, 1), 1, 254)
    codes = (b * np.exp2(127.0 - byte)[:, None, :]).reshape(r, m).astype(np.float32).astype(ml_dtypes.float8_e4m3fn).view(np.uint8)
    words = codes.reshape(r // 512, 128, 4, m).transpose(0, 1, 3, 2)
    return np.ascontiguousarray(words), np.ascontiguousarray(byte.astype(np.uint8).reshape(r // 512, 16, m))


B, N, T, D, NQ = 1, 512, 2048, 512, 512


def setup_inputs():
    n = np.random.standard_normal
    pages = np.random.permutation(T // 32)[:B * N // 32]
    idx = (pages[:, None] * 32 + np.arange(32)[None, :]).reshape(-1)
    s = mx_kscale(D)[:, None]
    kp = pack_weight(n((D, T)) / s, "e4m3")
    return {
        "qT": (n((B, D, NQ)) * s * (1.00 / np.sqrt(D))).astype(np.float32),
        "k_words": kp[0],
        "k_scales": kp[1],
        "ls": (np.random.uniform(7.8, 8.4, (B, 1, NQ))).astype(np.float32),
        "offs": striped(idx),
    }


def reference(qT, k_words, k_scales, ls, offs):
    idx = unstriped(offs)
    pick = lambda x, which: x[:, which].reshape(x.shape[0], B, -1).transpose(1, 0, 2)
    k = unpack_weight(k_words, k_scales, "e4m3")
    kg = pick(k, idx)
    qq = mxq(f64(qT), 1, "e4m3")
    a = kg.transpose(0, 2, 1) @ qq
    y = np.exp(a - f64(ls))
    Y = y[0]
    words, scales = planes(Y)
    return Y, words, scales

@@ -1,0 +1,189 @@
+from contextlib import ExitStack
+
+import concourse.mybir as mybir
+from concourse.masks import make_identity
+
+F32 = mybir.dt.float32
+BF16 = mybir.dt.bfloat16
+I32 = mybir.dt.int32
+U32 = mybir.dt.uint32
+U16 = mybir.dt.uint16
+U8 = mybir.dt.uint8
+FP8X4 = mybir.dt.float8_e4m3fn_x4
+EXP = mybir.ActivationFunctionType.Exp
+SUB = mybir.AluOpType.subtract
+
+P = 128
+PACK = 4
+N, T, D, NQ = 512, 2048, 512, 512
+HALF = NQ // 2
+CH = 128
+FLOPS = 2 * N * D * NQ
+
+
+def woven(dst):
+    return dst.rearrange("p (c i) t -> p c t i", i=4)
+
+
+def planar(src):
+    return src.rearrange("p t (c i) -> p c t i", i=4)
+
+
+def tile_attend_plw_soft_kernel(tc, qT, k_words, k_scales, ls, offs, out_0, out_1, out_2):
+    nc = tc.nc
+    with ExitStack() as ctx:
+        keep = ctx.enter_context(tc.tile_pool(name="keep", bufs=1))
+        psum = ctx.enter_context(tc.psum_pool(name="psum", bufs=1))
+
+        q_rows = qT[0].rearrange("(p j) q -> p j q", j=PACK)
+        y_rows = out_0.rearrange("(p r) q -> p r q", r=PACK)
+        y_words = out_1[0].rearrange("p q u -> p (q u)").bitcast(I32)
+        chunks = NQ // CH
+
+        offsets = keep.tile([P, N // 16], U16, name="offsets")
+        pool_words = keep.tile([P, T], U32, name="pool_words", align_bytes=64)
+        pool_scales = keep.tile([P, T], U8, name="pool_scales", align_bytes=64)
+        ls_cols = keep.tile([P, PACK], F32, name="ls_cols")
+        q_raw = [keep.tile([P, PACK, HALF], F32, name="q_raw%d" % h, align_bytes=64) for h in range(2)]
+        warm_in = keep.tile([P, 1], F32, name="warm_in")
+        warm_out = keep.tile([P, 1], F32, name="warm_out")
+        ident = keep.tile([P, P], F32, name="ident")
+        ls_bank = psum.tile([P, PACK, P], F32, name="ls_bank")
+        ls_rows = keep.tile([P, NQ], F32, name="ls_rows", align_bytes=64)
+        got_scales = keep.tile([P, N], U8, name="got_scales", align_bytes=64)
+        k_plane = keep.tile([P, N], U8, name="k_plane", align_bytes=64)
+        k_codes = keep.tile([P, N], U32, name="k_codes", align_bytes=64)
+        q_bf = [keep.tile([P, CH, PACK], BF16, name="q_bf%d" % c, align_bytes=64) for c in range(chunks)]
+        q_codes = [keep.tile([P, CH], U32, name="q_codes%d" % c, align_bytes=64) for c in range(chunks)]
+        q_plane = [keep.tile([P, CH], U8, name="q_plane%d" % c, align_bytes=64) for c in range(chunks)]
+        y_codes = keep.tile([P, NQ], U32, name="y_codes", align_bytes=64)
+        y_plane = keep.tile([P, NQ], U8, name="y_plane", align_bytes=64)
+        banks = [psum.tile([P, PACK, CH], F32, name="bank%d" % c) for c in range(chunks)]
+        shifted = [keep.tile([P, PACK, CH], F32, name="shifted%d" % c, align_bytes=64) for c in range(chunks)]
+        y = [keep.tile([P, PACK, CH], F32, name="y%d" % c, align_bytes=64) for c in range(chunks)]
+        y_bf = [keep.tile([P, CH, PACK], BF16, name="y_bf%d" % c, align_bytes=64) for c in range(chunks)]
+
+        def load_scales(queue, quad):
+            queue.dma_start(
+                pool_scales[32 * quad : 32 * quad + 4, :].bitcast(I32),
+                k_scales[0, 4 * quad : 4 * quad + 4, :].bitcast(I32),
+            )
+
+        def round_q(copy, c):
+            cols = slice((c % 2) * CH, (c % 2 + 1) * CH)
+            copy(woven(q_bf[c][:]), planar(q_raw[c // 2][:, :, cols]))
+
+        def quantise_q(c):
+            nc.vector.quantize_mx(
+                out=q_codes[c][:].bitcast(FP8X4),
+                scales=q_plane[c][:],
+                in_=q_bf[c][:].rearrange("p q j -> p (q j)"),
+            )
+
+        def scores(c):
+            for r in range(PACK):
+                nc.tensor.matmul_mx(
+                    out=banks[c][:, r, :],
+                    lhsT=k_codes[:, r * P : (r + 1) * P].bitcast(FP8X4),
+                    lhsT_scale=k_plane[:, r * P : (r + 1) * P],
+                    rhs=q_codes[c][:].bitcast(FP8X4),
+                    rhs_scale=q_plane[c][:],
+                    start=True,
+                    stop=True,
+                )
+
+        def shift(c):
+            nc.vector.tensor_tensor(
+                shifted[c][:],
+                banks[c][:],
+                ls_rows[:, c * CH : (c + 1) * CH].unsqueeze(1).to_broadcast([P, PACK, CH]),
+                SUB,
+            )
+
+        def weights(c):
+            nc.scalar.activation(y[c][:], shifted[c][:], EXP)
+            nc.sync.dma_start(y_rows[:, :, c * CH : (c + 1) * CH], y[c][:])
+
+        def round_y(copy, c):
+            copy(woven(y_bf[c][:]), planar(y[c][:]))
+
+        def quantise_y(c):
+            cols = slice(c * CH, (c + 1) * CH)
+            nc.vector.quantize_mx(
+                out=y_codes[:, cols].bitcast(FP8X4),
+                scales=y_plane[:, cols],
+                in_=y_bf[c][:].rearrange("p q u -> p (q u)"),
+            )
+
+        def store_words(a, b):
+            nc.sync.dma_start(y_words[:, a:b], y_codes[:, a:b].bitcast(I32))
+
+        def store_scales(queue, quad):
+            queue.dma_start(
+                out_2[0, 4 * quad : 4 * quad + 4, :].bitcast(I32),
+                y_plane[32 * quad : 32 * quad + 4, :].bitcast(I32),
+            )
+
+        def spread_ls():
+            make_identity(nc, ident[:])
+            for j in range(PACK):
+                nc.tensor.transpose(ls_bank[:, j, :], ls_cols[:, j : j + 1].to_broadcast([P, P]), ident[:])
+            nc.scalar.copy(ls_rows[:].rearrange("p (n j) -> p n j", j=PACK), ls_bank[:].rearrange("p j n -> p n j"))
+
+        vcopy = nc.vector.tensor_copy
+        scopy = nc.scalar.copy
+
+        k_rows = k_words[0].rearrange("p t r -> p (t r)").bitcast(I32)
+        nc.vector.memset(pool_scales[:, 0 : T // 2].bitcast(I32), 0)
+        nc.gpsimd.memset(pool_scales[:, T // 2 : T].bitcast(I32), 0)
+        nc.vector.memset(warm_in[:], 0.0)
+        nc.sync.dma_start(offsets[:], offs)
+        nc.sync.dma_start(pool_words[:, 0:512].bitcast(I32), k_rows[:, 0:512])
+        for quad in range(4):
+            load_scales(nc.sync, quad)
+        nc.sync.dma_start(ls_cols[:], ls[0, 0].rearrange("(p j) -> p j", j=PACK))
+        nc.sync.dma_start(pool_words[:, 512:T].bitcast(I32), k_rows[:, 512:T])
+        nc.sync.dma_start(q_raw[0][:], q_rows[:, :, 0:HALF])
+        nc.sync.dma_start(q_raw[1][:], q_rows[:, :, HALF:NQ])
+        nc.scalar.activation(warm_out[:], warm_in[:], EXP)
+        spread_ls()
+
+        vcopy(got_scales[:], pool_scales[:].indirect(offsets[:]))
+        vcopy(k_plane[:].rearrange("p (r s) -> p r s", r=PACK), got_scales[:].rearrange("p (s r) -> p r s", r=PACK))
+        vcopy(k_codes[:].rearrange("p (r s) -> p s r", r=PACK), pool_words[:].indirect(offsets[:]))
+
+        round_q(vcopy, 0)
+        round_q(scopy, 1)
+        quantise_q(0)
+        scores(0)
+        quantise_q(1)
+        scores(1)
+        round_q(vcopy, 2)
+        round_q(scopy, 3)
+        quantise_q(2)
+        scores(2)
+        quantise_q(3)
+        scores(3)
+        shift(0)
+        weights(0)
+        shift(1)
+        weights(1)
+        shift(2)
+        weights(2)
+        shift(3)
+        weights(3)
+        round_y(vcopy, 0)
+        round_y(vcopy, 1)
+        quantise_y(0)
+        round_y(vcopy, 2)
+        round_y(scopy, 3)
+        quantise_y(1)
+        store_words(0, HALF)
+        quantise_y(2)
+        store_words(HALF, HALF + CH)
+        quantise_y(3)
+        store_words(HALF + CH, NQ)
+        store_scales(nc.scalar, 0)
+        store_scales(nc.scalar, 1)
+        store_scales(nc.sync, 2)
+        store_scales(nc.scalar, 3)

@@ -1,7 +1,6 @@
 from contextlib import ExitStack
 
 import concourse.mybir as mybir
-from concourse.masks import make_identity
 
 F32 = mybir.dt.float32
 BF16 = mybir.dt.bfloat16
@@ -12,6 +11,9 @@ U8 = mybir.dt.uint8
 FP8X4 = mybir.dt.float8_e4m3fn_x4
 EXP = mybir.ActivationFunctionType.Exp
 SUB = mybir.AluOpType.subtract
+ADD = mybir.AluOpType.add
+MULT = mybir.AluOpType.mult
+EQUAL = mybir.AluOpType.is_equal
 
 P = 128
 PACK = 4
@@ -44,7 +46,7 @@ def tile_attend_plw_soft_kernel(tc, qT, k_words, k_scales, ls, offs, out_0, out_
         pool_words = keep.tile([P, T], U32, name="pool_words", align_bytes=64)
         pool_scales = keep.tile([P, T], U8, name="pool_scales", align_bytes=64)
         ls_cols = keep.tile([P, PACK], F32, name="ls_cols")
-        q_raw = [keep.tile([P, PACK, HALF], F32, name="q_raw%d" % h, align_bytes=64) for h in range(2)]
+        q_raw = [keep.tile([P, PACK, CH], F32, name="q_raw%d" % c, tag="stage%d" % c, align_bytes=64) for c in range(chunks)]
         warm_in = keep.tile([P, 1], F32, name="warm_in")
         warm_out = keep.tile([P, 1], F32, name="warm_out")
         ident = keep.tile([P, P], F32, name="ident")
@@ -59,7 +61,7 @@ def tile_attend_plw_soft_kernel(tc, qT, k_words, k_scales, ls, offs, out_0, out_
         y_codes = keep.tile([P, NQ], U32, name="y_codes", align_bytes=64)
         y_plane = keep.tile([P, NQ], U8, name="y_plane", align_bytes=64)
         banks = [psum.tile([P, PACK, CH], F32, name="bank%d" % c) for c in range(chunks)]
-        shifted = [keep.tile([P, PACK, CH], F32, name="shifted%d" % c, align_bytes=64) for c in range(chunks)]
+        shifted = [keep.tile([P, PACK, CH], F32, name="shifted%d" % c, tag="stage%d" % ((c + 2) % chunks), align_bytes=64) for c in range(chunks)]
         y = [keep.tile([P, PACK, CH], F32, name="y%d" % c, align_bytes=64) for c in range(chunks)]
         y_bf = [keep.tile([P, CH, PACK], BF16, name="y_bf%d" % c, align_bytes=64) for c in range(chunks)]
 
@@ -70,8 +72,7 @@ def tile_attend_plw_soft_kernel(tc, qT, k_words, k_scales, ls, offs, out_0, out_
             )
 
         def round_q(copy, c):
-            cols = slice((c % 2) * CH, (c % 2 + 1) * CH)
-            copy(woven(q_bf[c][:]), planar(q_raw[c // 2][:, :, cols]))
+            copy(woven(q_bf[c][:]), planar(q_raw[c][:]))
 
         def quantise_q(c):
             nc.vector.quantize_mx(
@@ -125,7 +126,16 @@ def tile_attend_plw_soft_kernel(tc, qT, k_words, k_scales, ls, offs, out_0, out_
             )
 
         def spread_ls():
-            make_identity(nc, ident[:])
+            ones = keep.tile([P, 32], F32, name="ones")
+            column = keep.tile([P, 32], F32, name="column", align_bytes=64)
+            row = keep.tile([P, 32], F32, name="row", align_bytes=64)
+            nc.vector.memset(ident[:], 0.0)
+            nc.vector.memset(ones[:], 1.0)
+            nc.vector.tensor_tensor_scan(column[:], ones[:], ones[:], 0.0, MULT, ADD)
+            nc.vector.transpose(row[:], column[:])
+            for quad in range(4):
+                part = slice(32 * quad, 32 * quad + 32)
+                nc.vector.tensor_tensor(ident[part, part], column[part, :], row[part, :], EQUAL)
             for j in range(PACK):
                 nc.tensor.transpose(ls_bank[:, j, :], ls_cols[:, j : j + 1].to_broadcast([P, P]), ident[:])
             nc.scalar.copy(ls_rows[:].rearrange("p (n j) -> p n j", j=PACK), ls_bank[:].rearrange("p j n -> p n j"))
@@ -134,17 +144,18 @@ def tile_attend_plw_soft_kernel(tc, qT, k_words, k_scales, ls, offs, out_0, out_
         scopy = nc.scalar.copy
 
         k_rows = k_words[0].rearrange("p t r -> p (t r)").bitcast(I32)
-        nc.vector.memset(pool_scales[:, 0 : T // 2].bitcast(I32), 0)
-        nc.gpsimd.memset(pool_scales[:, T // 2 : T].bitcast(I32), 0)
+        nc.vector.memset(pool_scales[:].bitcast(I32), 0)
         nc.vector.memset(warm_in[:], 0.0)
+        nc.sync.dma_start(pool_words[:, 0:640].bitcast(I32), k_rows[:, 0:640])
         nc.sync.dma_start(offsets[:], offs)
-        nc.sync.dma_start(pool_words[:, 0:512].bitcast(I32), k_rows[:, 0:512])
-        for quad in range(4):
-            load_scales(nc.sync, quad)
         nc.sync.dma_start(ls_cols[:], ls[0, 0].rearrange("(p j) -> p j", j=PACK))
-        nc.sync.dma_start(pool_words[:, 512:T].bitcast(I32), k_rows[:, 512:T])
-        nc.sync.dma_start(q_raw[0][:], q_rows[:, :, 0:HALF])
-        nc.sync.dma_start(q_raw[1][:], q_rows[:, :, HALF:NQ])
+        load_scales(nc.sync, 0)
+        load_scales(nc.scalar, 1)
+        load_scales(nc.sync, 2)
+        load_scales(nc.scalar, 3)
+        nc.sync.dma_start(pool_words[:, 640:T].bitcast(I32), k_rows[:, 640:T])
+        for c in range(chunks):
+            nc.sync.dma_start(q_raw[c][:], q_rows[:, :, c * CH : (c + 1) * CH])
         nc.scalar.activation(warm_out[:], warm_in[:], EXP)
         spread_ls()
 
@@ -152,38 +163,24 @@ def tile_attend_plw_soft_kernel(tc, qT, k_words, k_scales, ls, offs, out_0, out_
         vcopy(k_plane[:].rearrange("p (r s) -> p r s", r=PACK), got_scales[:].rearrange("p (s r) -> p r s", r=PACK))
         vcopy(k_codes[:].rearrange("p (r s) -> p s r", r=PACK), pool_words[:].indirect(offsets[:]))
 
-        round_q(vcopy, 0)
-        round_q(scopy, 1)
-        quantise_q(0)
-        scores(0)
-        quantise_q(1)
-        scores(1)
-        round_q(vcopy, 2)
-        round_q(scopy, 3)
-        quantise_q(2)
-        scores(2)
-        quantise_q(3)
-        scores(3)
-        shift(0)
-        weights(0)
-        shift(1)
-        weights(1)
-        shift(2)
-        weights(2)
-        shift(3)
-        weights(3)
+        for c in range(chunks):
+            round_q(scopy, c)
+            quantise_q(c)
+            scores(c)
+        for c in range(chunks):
+            shift(c)
+            weights(c)
+        nc.scalar.activation(woven(y_bf[3][:]), planar(shifted[3][:]), EXP)
         round_y(vcopy, 0)
         round_y(vcopy, 1)
         quantise_y(0)
         round_y(vcopy, 2)
-        round_y(scopy, 3)
         quantise_y(1)
         store_words(0, HALF)
         quantise_y(2)
-        store_words(HALF, HALF + CH)
         quantise_y(3)
-        store_words(HALF + CH, NQ)
+        store_words(HALF, NQ)
         store_scales(nc.scalar, 0)
-        store_scales(nc.scalar, 1)
-        store_scales(nc.sync, 2)
+        store_scales(nc.sync, 1)
+        store_scales(nc.scalar, 2)
         store_scales(nc.scalar, 3)

@@ -52,15 +52,16 @@ def tile_attend_plw_soft_kernel(tc, qT, k_words, k_scales, ls, offs, out_0, out_
         ident = keep.tile([P, P], F32, name="ident")
         ls_bank = psum.tile([P, PACK, P], F32, name="ls_bank")
         ls_rows = keep.tile([P, NQ], F32, name="ls_rows", align_bytes=64)
-        got_scales = keep.tile([P, N], U8, name="got_scales", align_bytes=64)
+        got_scales = keep.tile([P, N], U8, name="got_scales", tag="gathered", align_bytes=64)
         k_plane = keep.tile([P, N], U8, name="k_plane", align_bytes=64)
-        k_codes = keep.tile([P, N], U32, name="k_codes", align_bytes=64)
+        k_codes = keep.tile([P, N], U32, name="k_codes", tag="gathered", align_bytes=64)
         q_bf = [keep.tile([P, CH, PACK], BF16, name="q_bf%d" % c, align_bytes=64) for c in range(chunks)]
         q_codes = [keep.tile([P, CH], U32, name="q_codes%d" % c, align_bytes=64) for c in range(chunks)]
         q_plane = [keep.tile([P, CH], U8, name="q_plane%d" % c, align_bytes=64) for c in range(chunks)]
         y_codes = keep.tile([P, NQ], U32, name="y_codes", align_bytes=64)
         y_plane = keep.tile([P, NQ], U8, name="y_plane", align_bytes=64)
-        banks = [psum.tile([P, PACK, CH], F32, name="bank%d" % c) for c in range(chunks)]
+        parts = [(0, 0, 2), (0, 2, 4), (1, 0, 4), (2, 0, 4), (3, 0, 4)]
+        banks = [psum.tile([P, b - a, CH], F32, name="bank%d" % u) for u, (c, a, b) in enumerate(parts)]
         shifted = [keep.tile([P, PACK, CH], F32, name="shifted%d" % c, tag="stage%d" % ((c + 2) % chunks), align_bytes=64) for c in range(chunks)]
         y = [keep.tile([P, PACK, CH], F32, name="y%d" % c, align_bytes=64) for c in range(chunks)]
         y_bf = [keep.tile([P, CH, PACK], BF16, name="y_bf%d" % c, align_bytes=64) for c in range(chunks)]
@@ -81,10 +82,11 @@ def tile_attend_plw_soft_kernel(tc, qT, k_words, k_scales, ls, offs, out_0, out_
                 in_=q_bf[c][:].rearrange("p q j -> p (q j)"),
             )
 
-        def scores(c):
-            for r in range(PACK):
+        def scores(u):
+            c, a, b = parts[u]
+            for r in range(a, b):
                 nc.tensor.matmul_mx(
-                    out=banks[c][:, r, :],
+                    out=banks[u][:, r - a, :],
                     lhsT=k_codes[:, r * P : (r + 1) * P].bitcast(FP8X4),
                     lhsT_scale=k_plane[:, r * P : (r + 1) * P],
                     rhs=q_codes[c][:].bitcast(FP8X4),
@@ -93,17 +95,19 @@ def tile_attend_plw_soft_kernel(tc, qT, k_words, k_scales, ls, offs, out_0, out_
                     stop=True,
                 )
 
-        def shift(c):
+        def shift(u):
+            c, a, b = parts[u]
             nc.vector.tensor_tensor(
-                shifted[c][:],
-                banks[c][:],
-                ls_rows[:, c * CH : (c + 1) * CH].unsqueeze(1).to_broadcast([P, PACK, CH]),
+                shifted[c][:, a:b, :],
+                banks[u][:],
+                ls_rows[:, c * CH : (c + 1) * CH].unsqueeze(1).to_broadcast([P, b - a, CH]),
                 SUB,
             )
 
-        def weights(c):
-            nc.scalar.activation(y[c][:], shifted[c][:], EXP)
-            nc.sync.dma_start(y_rows[:, :, c * CH : (c + 1) * CH], y[c][:])
+        def weights(u):
+            c, a, b = parts[u]
+            nc.scalar.activation(y[c][:, a:b, :], shifted[c][:, a:b, :], EXP)
+            nc.sync.dma_start(y_rows[:, a:b, c * CH : (c + 1) * CH], y[c][:, a:b, :])
 
         def round_y(copy, c):
             copy(woven(y_bf[c][:]), planar(y[c][:]))
@@ -146,14 +150,14 @@ def tile_attend_plw_soft_kernel(tc, qT, k_words, k_scales, ls, offs, out_0, out_
         k_rows = k_words[0].rearrange("p t r -> p (t r)").bitcast(I32)
         nc.vector.memset(pool_scales[:].bitcast(I32), 0)
         nc.vector.memset(warm_in[:], 0.0)
-        nc.sync.dma_start(pool_words[:, 0:640].bitcast(I32), k_rows[:, 0:640])
+        nc.sync.dma_start(pool_words[:, 0:896].bitcast(I32), k_rows[:, 0:896])
         nc.sync.dma_start(offsets[:], offs)
         nc.sync.dma_start(ls_cols[:], ls[0, 0].rearrange("(p j) -> p j", j=PACK))
         load_scales(nc.sync, 0)
         load_scales(nc.scalar, 1)
         load_scales(nc.sync, 2)
         load_scales(nc.scalar, 3)
-        nc.sync.dma_start(pool_words[:, 640:T].bitcast(I32), k_rows[:, 640:T])
+        nc.sync.dma_start(pool_words[:, 896:T].bitcast(I32), k_rows[:, 896:T])
         for c in range(chunks):
             nc.sync.dma_start(q_raw[c][:], q_rows[:, :, c * CH : (c + 1) * CH])
         nc.scalar.activation(warm_out[:], warm_in[:], EXP)
@@ -166,10 +170,12 @@ def tile_attend_plw_soft_kernel(tc, qT, k_words, k_scales, ls, offs, out_0, out_
         for c in range(chunks):
             round_q(scopy, c)
             quantise_q(c)
-            scores(c)
-        for c in range(chunks):
-            shift(c)
-            weights(c)
+            for u, part in enumerate(parts):
+                if part[0] == c:
+                    scores(u)
+        for u in range(len(parts)):
+            shift(u)
+            weights(u)
         nc.scalar.activation(woven(y_bf[3][:]), planar(shifted[3][:]), EXP)
         round_y(vcopy, 0)
         round_y(vcopy, 1)

@@ -47,8 +47,6 @@ def tile_attend_plw_soft_kernel(tc, qT, k_words, k_scales, ls, offs, out_0, out_
         pool_scales = keep.tile([P, T], U8, name="pool_scales", align_bytes=64)
         ls_cols = keep.tile([P, PACK], F32, name="ls_cols")
         q_raw = [keep.tile([P, PACK, CH], F32, name="q_raw%d" % c, tag="stage%d" % c, align_bytes=64) for c in range(chunks)]
-        warm_in = keep.tile([P, 1], F32, name="warm_in")
-        warm_out = keep.tile([P, 1], F32, name="warm_out")
         ident = keep.tile([P, P], F32, name="ident")
         ls_bank = psum.tile([P, PACK, P], F32, name="ls_bank")
         ls_rows = keep.tile([P, NQ], F32, name="ls_rows", align_bytes=64)
@@ -149,7 +147,6 @@ def tile_attend_plw_soft_kernel(tc, qT, k_words, k_scales, ls, offs, out_0, out_
 
         k_rows = k_words[0].rearrange("p t r -> p (t r)").bitcast(I32)
         nc.vector.memset(pool_scales[:].bitcast(I32), 0)
-        nc.vector.memset(warm_in[:], 0.0)
         nc.sync.dma_start(pool_words[:, 0:896].bitcast(I32), k_rows[:, 0:896])
         nc.sync.dma_start(offsets[:], offs)
         nc.sync.dma_start(ls_cols[:], ls[0, 0].rearrange("(p j) -> p j", j=PACK))
@@ -160,7 +157,6 @@ def tile_attend_plw_soft_kernel(tc, qT, k_words, k_scales, ls, offs, out_0, out_
         nc.sync.dma_start(pool_words[:, 896:T].bitcast(I32), k_rows[:, 896:T])
         for c in range(chunks):
             nc.sync.dma_start(q_raw[c][:], q_rows[:, :, c * CH : (c + 1) * CH])
-        nc.scalar.activation(warm_out[:], warm_in[:], EXP)
         spread_ls()
 
         vcopy(got_scales[:], pool_scales[:].indirect(offsets[:]))

@@ -38,31 +38,45 @@ def tile_attend_plw_soft_kernel(tc, qT, k_words, k_scales, ls, offs, out_0, out_
         psum = ctx.enter_context(tc.psum_pool(name="psum", bufs=1))
 
         q_rows = qT[0].rearrange("(p j) q -> p j q", j=PACK)
+        k_rows = k_words[0].rearrange("p t r -> p (t r)").bitcast(I32)
         y_rows = out_0.rearrange("(p r) q -> p r q", r=PACK)
         y_words = out_1[0].rearrange("p q u -> p (q u)").bitcast(I32)
-        chunks = NQ // CH
 
         offsets = keep.tile([P, N // 16], U16, name="offsets")
         pool_words = keep.tile([P, T], U32, name="pool_words", align_bytes=64)
-        pool_scales = keep.tile([P, T], U8, name="pool_scales", align_bytes=64)
+        pool_scales = keep.tile([P, T], U8, name="pool_scales", tag="window", align_bytes=64)
         ls_cols = keep.tile([P, PACK], F32, name="ls_cols")
-        q_raw = [keep.tile([P, PACK, CH], F32, name="q_raw%d" % c, tag="stage%d" % c, align_bytes=64) for c in range(chunks)]
         ident = keep.tile([P, P], F32, name="ident")
-        ls_bank = psum.tile([P, PACK, P], F32, name="ls_bank")
+        ls_bank = psum.tile([P, PACK, P], F32, name="ls_bank", tag="turned")
         ls_rows = keep.tile([P, NQ], F32, name="ls_rows", align_bytes=64)
         got_scales = keep.tile([P, N], U8, name="got_scales", tag="gathered", align_bytes=64)
         k_plane = keep.tile([P, N], U8, name="k_plane", align_bytes=64)
         k_codes = keep.tile([P, N], U32, name="k_codes", tag="gathered", align_bytes=64)
-        q_bf = [keep.tile([P, CH, PACK], BF16, name="q_bf%d" % c, align_bytes=64) for c in range(chunks)]
-        q_codes = [keep.tile([P, CH], U32, name="q_codes%d" % c, align_bytes=64) for c in range(chunks)]
-        q_plane = [keep.tile([P, CH], U8, name="q_plane%d" % c, align_bytes=64) for c in range(chunks)]
+        pieces = [(0, 128), (128, 256), (256, 512)]
+        q_raw = [keep.tile([P, PACK, b - a], F32, name="q_raw%d" % h, tag="stage%d" % h, align_bytes=64) for h, (a, b) in enumerate(pieces)]
+        q_bf = [keep.tile([P, b - a, PACK], BF16, name="q_bf%d" % h, align_bytes=64) for h, (a, b) in enumerate(pieces)]
+        q_codes = [keep.tile([P, HALF], U32, name="q_codes%d" % h, tag="window" if h == 0 else "", align_bytes=64) for h in range(2)]
+        q_plane = [keep.tile([P, HALF], U8, name="q_plane%d" % h, align_bytes=64) for h in range(2)]
+        shifted = keep.tile([P, PACK, HALF], F32, name="shifted", align_bytes=64)
+        y = [keep.tile([P, PACK, HALF], F32, name="y%d" % h, align_bytes=64) for h in range(2)]
+        y_bf = [keep.tile([P, HALF, PACK], BF16, name="y_bf%d" % h, align_bytes=64) for h in range(2)]
         y_codes = keep.tile([P, NQ], U32, name="y_codes", align_bytes=64)
         y_plane = keep.tile([P, NQ], U8, name="y_plane", align_bytes=64)
-        parts = [(0, 0, 2), (0, 2, 4), (1, 0, 4), (2, 0, 4), (3, 0, 4)]
-        banks = [psum.tile([P, b - a, CH], F32, name="bank%d" % u) for u, (c, a, b) in enumerate(parts)]
-        shifted = [keep.tile([P, PACK, CH], F32, name="shifted%d" % c, tag="stage%d" % ((c + 2) % chunks), align_bytes=64) for c in range(chunks)]
-        y = [keep.tile([P, PACK, CH], F32, name="y%d" % c, align_bytes=64) for c in range(chunks)]
-        y_bf = [keep.tile([P, CH, PACK], BF16, name="y_bf%d" % c, align_bytes=64) for c in range(chunks)]
+        parts = [(r0, r0 + 2, a, a + CH) for a in range(0, NQ, CH) for r0 in (0, 2)]
+        banks = [
+            psum.tile([P, r1 - r0, b - a], F32, name="bank%d" % u, tag="turned" if u == len(parts) - 1 else "")
+            for u, (r0, r1, a, b) in enumerate(parts)
+        ]
+
+        def inside(a, b):
+            h = max(h for h, piece in enumerate(pieces) if piece[0] <= a)
+            return h, slice(a - pieces[h][0], b - pieces[h][0])
+
+        def in_half(a, b):
+            return a // HALF, slice(a % HALF, a % HALF + b - a)
+
+        def load_q(h):
+            nc.sync.dma_start(q_raw[h][:], q_rows[:, :, pieces[h][0] : pieces[h][1]])
 
         def load_scales(queue, quad):
             queue.dma_start(
@@ -70,52 +84,68 @@ def tile_attend_plw_soft_kernel(tc, qT, k_words, k_scales, ls, offs, out_0, out_
                 k_scales[0, 4 * quad : 4 * quad + 4, :].bitcast(I32),
             )
 
-        def round_q(copy, c):
-            copy(woven(q_bf[c][:]), planar(q_raw[c][:]))
+        def round_q(copy, a, b):
+            h, cols = inside(a, b)
+            copy(woven(q_bf[h][:, cols, :]), planar(q_raw[h][:, :, cols]))
 
-        def quantise_q(c):
+        def quantise_q(a, b):
+            h, cols = inside(a, b)
+            half, codes = in_half(a, b)
             nc.vector.quantize_mx(
-                out=q_codes[c][:].bitcast(FP8X4),
-                scales=q_plane[c][:],
-                in_=q_bf[c][:].rearrange("p q j -> p (q j)"),
+                out=q_codes[half][:, codes].bitcast(FP8X4),
+                scales=q_plane[half][:, codes],
+                in_=q_bf[h][:, cols, :].rearrange("p q j -> p (q j)"),
             )
 
         def scores(u):
-            c, a, b = parts[u]
-            for r in range(a, b):
+            r0, r1, a, b = parts[u]
+            h, cols = in_half(a, b)
+            for r in range(r0, r1):
                 nc.tensor.matmul_mx(
-                    out=banks[u][:, r - a, :],
+                    out=banks[u][:, r - r0, :],
                     lhsT=k_codes[:, r * P : (r + 1) * P].bitcast(FP8X4),
                     lhsT_scale=k_plane[:, r * P : (r + 1) * P],
-                    rhs=q_codes[c][:].bitcast(FP8X4),
-                    rhs_scale=q_plane[c][:],
+                    rhs=q_codes[h][:, cols].bitcast(FP8X4),
+                    rhs_scale=q_plane[h][:, cols],
                     start=True,
                     stop=True,
                 )
 
+        staged = [q_raw[2][:, :, CH:HALF], q_raw[2][:, :, 0:CH], shifted[:, :, 0:CH], shifted[:, :, CH:HALF]]
+
         def shift(u):
-            c, a, b = parts[u]
+            r0, r1, a, b = parts[u]
             nc.vector.tensor_tensor(
-                shifted[c][:, a:b, :],
+                staged[a // CH][:, r0:r1, :],
                 banks[u][:],
-                ls_rows[:, c * CH : (c + 1) * CH].unsqueeze(1).to_broadcast([P, b - a, CH]),
+                ls_rows[:, a:b].unsqueeze(1).to_broadcast([P, r1 - r0, b - a]),
                 SUB,
             )
 
         def weights(u):
-            c, a, b = parts[u]
-            nc.scalar.activation(y[c][:, a:b, :], shifted[c][:, a:b, :], EXP)
-            nc.sync.dma_start(y_rows[:, a:b, c * CH : (c + 1) * CH], y[c][:, a:b, :])
+            r0, r1, a, b = parts[u]
+            h, cols = in_half(a, b)
+            nc.scalar.activation(y[h][:, r0:r1, cols], staged[a // CH][:, r0:r1, :], EXP)
+            if b % HALF == 0:
+                store_weights(h, r0, r1)
 
-        def round_y(copy, c):
-            copy(woven(y_bf[c][:]), planar(y[c][:]))
+        def store_weights(h, r0, r1):
+            nc.sync.dma_start(y_rows[:, r0:r1, h * HALF : (h + 1) * HALF], y[h][:, r0:r1, :])
 
-        def quantise_y(c):
-            cols = slice(c * CH, (c + 1) * CH)
+        def round_y(a, b):
+            h, cols = in_half(a, b)
+            nc.vector.tensor_copy(woven(y_bf[h][:, cols, :]), planar(y[h][:, :, cols]))
+
+        def weights_bf(a, b):
+            h, cols = in_half(a, b)
+            nc.scalar.activation(woven(y_bf[h][:, cols, :]), planar(staged[a // CH][:, :, a % CH : a % CH + b - a]), EXP)
+
+        def quantise_y(a, b):
+            h, cols = in_half(a, b)
             nc.vector.quantize_mx(
-                out=y_codes[:, cols].bitcast(FP8X4),
-                scales=y_plane[:, cols],
-                in_=y_bf[c][:].rearrange("p q u -> p (q u)"),
+                out=y_codes[:, a:b].bitcast(FP8X4),
+                scales=y_plane[:, a:b],
+                in_=y_bf[h][:, cols, :].rearrange("p q u -> p (q u)"),
             )
 
         def store_words(a, b):
@@ -145,42 +175,47 @@ def tile_attend_plw_soft_kernel(tc, qT, k_words, k_scales, ls, offs, out_0, out_
         vcopy = nc.vector.tensor_copy
         scopy = nc.scalar.copy
 
-        k_rows = k_words[0].rearrange("p t r -> p (t r)").bitcast(I32)
         nc.vector.memset(pool_scales[:].bitcast(I32), 0)
-        nc.sync.dma_start(pool_words[:, 0:896].bitcast(I32), k_rows[:, 0:896])
+        load_q(0)
         nc.sync.dma_start(offsets[:], offs)
         nc.sync.dma_start(ls_cols[:], ls[0, 0].rearrange("(p j) -> p j", j=PACK))
         load_scales(nc.sync, 0)
         load_scales(nc.scalar, 1)
         load_scales(nc.sync, 2)
         load_scales(nc.scalar, 3)
-        nc.sync.dma_start(pool_words[:, 896:T].bitcast(I32), k_rows[:, 896:T])
-        for c in range(chunks):
-            nc.sync.dma_start(q_raw[c][:], q_rows[:, :, c * CH : (c + 1) * CH])
+        nc.sync.dma_start(pool_words[:].bitcast(I32), k_rows)
+        load_q(1)
+        load_q(2)
         spread_ls()
 
+        round_q(scopy, 0, 128)
         vcopy(got_scales[:], pool_scales[:].indirect(offsets[:]))
         vcopy(k_plane[:].rearrange("p (r s) -> p r s", r=PACK), got_scales[:].rearrange("p (s r) -> p r s", r=PACK))
+        quantise_q(0, 128)
         vcopy(k_codes[:].rearrange("p (r s) -> p s r", r=PACK), pool_words[:].indirect(offsets[:]))
-
-        for c in range(chunks):
-            round_q(scopy, c)
-            quantise_q(c)
-            for u, part in enumerate(parts):
-                if part[0] == c:
-                    scores(u)
-        for u in range(len(parts)):
+        scores(0)
+        scores(1)
+        round_q(scopy, 128, 256)
+        quantise_q(128, 256)
+        scores(2)
+        scores(3)
+        round_q(scopy, 256, 352)
+        round_q(vcopy, 352, 512)
+        shift(0)
+        weights(0)
+        quantise_q(256, 512)
+        for u in range(4, 8):
+            scores(u)
+        for u in range(1, 8):
             shift(u)
             weights(u)
-        nc.scalar.activation(woven(y_bf[3][:]), planar(shifted[3][:]), EXP)
-        round_y(vcopy, 0)
-        round_y(vcopy, 1)
-        quantise_y(0)
-        round_y(vcopy, 2)
-        quantise_y(1)
+        round_y(0, 256)
+        weights_bf(384, 512)
+        round_y(256, 384)
+        quantise_y(0, 256)
         store_words(0, HALF)
-        quantise_y(2)
-        quantise_y(3)
+        quantise_y(256, 384)
+        quantise_y(384, 512)
         store_words(HALF, NQ)
         store_scales(nc.scalar, 0)
         store_scales(nc.sync, 1)

@@ -41,42 +41,41 @@ def tile_attend_plw_soft_kernel(tc, qT, k_words, k_scales, ls, offs, out_0, out_
         k_rows = k_words[0].rearrange("p t r -> p (t r)").bitcast(I32)
         y_rows = out_0.rearrange("(p r) q -> p r q", r=PACK)
         y_words = out_1[0].rearrange("p q u -> p (q u)").bitcast(I32)
+        chunks = NQ // CH
+
+        def sbuf(shape, dtype, name, tag=""):
+            return keep.tile(shape, dtype, name=name, tag=tag, align_bytes=64)
 
         offsets = keep.tile([P, N // 16], U16, name="offsets")
-        pool_words = keep.tile([P, T], U32, name="pool_words", align_bytes=64)
-        pool_scales = keep.tile([P, T], U8, name="pool_scales", tag="window", align_bytes=64)
+        pool_words = sbuf([P, T], U32, "pool_words")
+        pool_scales = sbuf([P, T], U8, "pool_scales", "window")
         ls_cols = keep.tile([P, PACK], F32, name="ls_cols")
         ident = keep.tile([P, P], F32, name="ident")
         ls_bank = psum.tile([P, PACK, P], F32, name="ls_bank", tag="turned")
-        ls_rows = keep.tile([P, NQ], F32, name="ls_rows", align_bytes=64)
-        got_scales = keep.tile([P, N], U8, name="got_scales", tag="gathered", align_bytes=64)
-        k_plane = keep.tile([P, N], U8, name="k_plane", align_bytes=64)
-        k_codes = keep.tile([P, N], U32, name="k_codes", tag="gathered", align_bytes=64)
-        pieces = [(0, 128), (128, 256), (256, 512)]
-        q_raw = [keep.tile([P, PACK, b - a], F32, name="q_raw%d" % h, tag="stage%d" % h, align_bytes=64) for h, (a, b) in enumerate(pieces)]
-        q_bf = [keep.tile([P, b - a, PACK], BF16, name="q_bf%d" % h, align_bytes=64) for h, (a, b) in enumerate(pieces)]
-        q_codes = [keep.tile([P, HALF], U32, name="q_codes%d" % h, tag="window" if h == 0 else "", align_bytes=64) for h in range(2)]
-        q_plane = [keep.tile([P, HALF], U8, name="q_plane%d" % h, align_bytes=64) for h in range(2)]
-        shifted = keep.tile([P, PACK, HALF], F32, name="shifted", align_bytes=64)
-        y = [keep.tile([P, PACK, HALF], F32, name="y%d" % h, align_bytes=64) for h in range(2)]
-        y_bf = [keep.tile([P, HALF, PACK], BF16, name="y_bf%d" % h, align_bytes=64) for h in range(2)]
-        y_codes = keep.tile([P, NQ], U32, name="y_codes", align_bytes=64)
-        y_plane = keep.tile([P, NQ], U8, name="y_plane", align_bytes=64)
-        parts = [(r0, r0 + 2, a, a + CH) for a in range(0, NQ, CH) for r0 in (0, 2)]
+        ls_rows = sbuf([P, NQ], F32, "ls_rows")
+        got_scales = sbuf([P, N], U8, "got_scales")
+        k_plane = sbuf([P, N], U8, "k_plane")
+        k_codes = sbuf([P, N], U32, "k_codes")
+        pieces = [(0, 128), (128, 384), (384, 512)]
+        q_raw = [sbuf([P, PACK, b - a], F32, "q_raw%d" % i, "raw%d" % i) for i, (a, b) in enumerate(pieces)]
+        q_bf = [sbuf([P, CH, PACK], BF16, "q_bf%d" % c, "stage%d" % c) for c in range(chunks)]
+        q_codes = [sbuf([P, b - a], U32, "q_codes%d" % i, "window" if i == 0 else "") for i, (a, b) in enumerate(pieces)]
+        q_plane = [sbuf([P, b - a], U8, "q_plane%d" % i) for i, (a, b) in enumerate(pieces)]
+        shifted = [sbuf([P, PACK, b - a], F32, "shifted%d" % i, ("stage1", "", "stage3")[i]) for i, (a, b) in enumerate(pieces)]
+        y = sbuf([P, PACK, NQ], F32, "y", "raw2")
+        y_bf = sbuf([P, NQ, PACK], BF16, "y_bf")
+        y_codes = sbuf([P, NQ], U32, "y_codes")
+        y_plane = sbuf([P, NQ], U8, "y_plane")
+        parts = [(0, 0, 2), (0, 2, 4), (1, 0, 1), (1, 1, 2), (1, 2, 3), (1, 3, 4), (2, 0, 2), (2, 2, 4)]
         banks = [
-            psum.tile([P, r1 - r0, b - a], F32, name="bank%d" % u, tag="turned" if u == len(parts) - 1 else "")
-            for u, (r0, r1, a, b) in enumerate(parts)
+            psum.tile([P, r1 - r0, pieces[i][1] - pieces[i][0]], F32, name="bank%d" % u, tag="turned" if u == len(parts) - 1 else "")
+            for u, (i, r0, r1) in enumerate(parts)
         ]
 
-        def inside(a, b):
-            h = max(h for h, piece in enumerate(pieces) if piece[0] <= a)
-            return h, slice(a - pieces[h][0], b - pieces[h][0])
-
-        def in_half(a, b):
-            return a // HALF, slice(a % HALF, a % HALF + b - a)
-
-        def load_q(h):
-            nc.sync.dma_start(q_raw[h][:], q_rows[:, :, pieces[h][0] : pieces[h][1]])
+        def piece_of(c):
+            i = max(i for i, piece in enumerate(pieces) if piece[0] <= c * CH)
+            a = c * CH - pieces[i][0]
+            return i, slice(a, a + CH)
 
         def load_scales(queue, quad):
             queue.dma_start(
@@ -84,68 +83,57 @@ def tile_attend_plw_soft_kernel(tc, qT, k_words, k_scales, ls, offs, out_0, out_
                 k_scales[0, 4 * quad : 4 * quad + 4, :].bitcast(I32),
             )
 
-        def round_q(copy, a, b):
-            h, cols = inside(a, b)
-            copy(woven(q_bf[h][:, cols, :]), planar(q_raw[h][:, :, cols]))
+        def load_q(i):
+            nc.sync.dma_start(q_raw[i][:], q_rows[:, :, pieces[i][0] : pieces[i][1]])
 
-        def quantise_q(a, b):
-            h, cols = inside(a, b)
-            half, codes = in_half(a, b)
+        def round_q(copy, c):
+            i, cols = piece_of(c)
+            copy(woven(q_bf[c][:]), planar(q_raw[i][:, :, cols]))
+
+        def quantise_q(c):
+            i, cols = piece_of(c)
             nc.vector.quantize_mx(
-                out=q_codes[half][:, codes].bitcast(FP8X4),
-                scales=q_plane[half][:, codes],
-                in_=q_bf[h][:, cols, :].rearrange("p q j -> p (q j)"),
+                out=q_codes[i][:, cols].bitcast(FP8X4),
+                scales=q_plane[i][:, cols],
+                in_=q_bf[c][:].rearrange("p q j -> p (q j)"),
             )
 
         def scores(u):
-            r0, r1, a, b = parts[u]
-            h, cols = in_half(a, b)
+            i, r0, r1 = parts[u]
             for r in range(r0, r1):
                 nc.tensor.matmul_mx(
                     out=banks[u][:, r - r0, :],
                     lhsT=k_codes[:, r * P : (r + 1) * P].bitcast(FP8X4),
                     lhsT_scale=k_plane[:, r * P : (r + 1) * P],
-                    rhs=q_codes[h][:, cols].bitcast(FP8X4),
-                    rhs_scale=q_plane[h][:, cols],
+                    rhs=q_codes[i][:].bitcast(FP8X4),
+                    rhs_scale=q_plane[i][:],
                     start=True,
                     stop=True,
                 )
 
-        staged = [q_raw[2][:, :, CH:HALF], q_raw[2][:, :, 0:CH], shifted[:, :, 0:CH], shifted[:, :, CH:HALF]]
-
-        def shift(u):
-            r0, r1, a, b = parts[u]
+        def weights(u):
+            i, r0, r1 = parts[u]
+            a, b = pieces[i]
             nc.vector.tensor_tensor(
-                staged[a // CH][:, r0:r1, :],
+                shifted[i][:, r0:r1, :],
                 banks[u][:],
                 ls_rows[:, a:b].unsqueeze(1).to_broadcast([P, r1 - r0, b - a]),
                 SUB,
             )
+            nc.scalar.activation(y[:, r0:r1, a:b], shifted[i][:, r0:r1, :], EXP)
 
-        def weights(u):
-            r0, r1, a, b = parts[u]
-            h, cols = in_half(a, b)
-            nc.scalar.activation(y[h][:, r0:r1, cols], staged[a // CH][:, r0:r1, :], EXP)
-            if b % HALF == 0:
-                store_weights(h, r0, r1)
-
-        def store_weights(h, r0, r1):
-            nc.sync.dma_start(y_rows[:, r0:r1, h * HALF : (h + 1) * HALF], y[h][:, r0:r1, :])
+        def store_weights(i, r0, r1):
+            a, b = pieces[i]
+            nc.sync.dma_start(y_rows[:, r0:r1, a:b], y[:, r0:r1, a:b])
 
         def round_y(a, b):
-            h, cols = in_half(a, b)
-            nc.vector.tensor_copy(woven(y_bf[h][:, cols, :]), planar(y[h][:, :, cols]))
-
-        def weights_bf(a, b):
-            h, cols = in_half(a, b)
-            nc.scalar.activation(woven(y_bf[h][:, cols, :]), planar(staged[a // CH][:, :, a % CH : a % CH + b - a]), EXP)
+            nc.vector.tensor_copy(woven(y_bf[:, a:b, :]), planar(y[:, :, a:b]))
 
         def quantise_y(a, b):
-            h, cols = in_half(a, b)
             nc.vector.quantize_mx(
                 out=y_codes[:, a:b].bitcast(FP8X4),
                 scales=y_plane[:, a:b],
-                in_=y_bf[h][:, cols, :].rearrange("p q u -> p (q u)"),
+                in_=y_bf[:, a:b, :].rearrange("p q u -> p (q u)"),
             )
 
         def store_words(a, b):
@@ -159,8 +147,8 @@ def tile_attend_plw_soft_kernel(tc, qT, k_words, k_scales, ls, offs, out_0, out_
 
         def spread_ls():
             ones = keep.tile([P, 32], F32, name="ones")
-            column = keep.tile([P, 32], F32, name="column", align_bytes=64)
-            row = keep.tile([P, 32], F32, name="row", align_bytes=64)
+            column = sbuf([P, 32], F32, "column")
+            row = sbuf([P, 32], F32, "row")
             nc.vector.memset(ident[:], 0.0)
             nc.vector.memset(ones[:], 1.0)
             nc.vector.tensor_tensor_scan(column[:], ones[:], ones[:], 0.0, MULT, ADD)
@@ -179,44 +167,53 @@ def tile_attend_plw_soft_kernel(tc, qT, k_words, k_scales, ls, offs, out_0, out_
         load_q(0)
         nc.sync.dma_start(offsets[:], offs)
         nc.sync.dma_start(ls_cols[:], ls[0, 0].rearrange("(p j) -> p j", j=PACK))
-        load_scales(nc.sync, 0)
-        load_scales(nc.scalar, 1)
-        load_scales(nc.sync, 2)
-        load_scales(nc.scalar, 3)
+        for quad in range(4):
+            load_scales(nc.scalar if quad % 2 else nc.sync, quad)
         nc.sync.dma_start(pool_words[:].bitcast(I32), k_rows)
-        load_q(1)
-        load_q(2)
+        for i in range(1, len(pieces)):
+            load_q(i)
         spread_ls()
 
-        round_q(scopy, 0, 128)
+        round_q(scopy, 0)
         vcopy(got_scales[:], pool_scales[:].indirect(offsets[:]))
+        quantise_q(0)
         vcopy(k_plane[:].rearrange("p (r s) -> p r s", r=PACK), got_scales[:].rearrange("p (s r) -> p r s", r=PACK))
-        quantise_q(0, 128)
         vcopy(k_codes[:].rearrange("p (r s) -> p s r", r=PACK), pool_words[:].indirect(offsets[:]))
+
         scores(0)
         scores(1)
-        round_q(scopy, 128, 256)
-        quantise_q(128, 256)
-        scores(2)
-        scores(3)
-        round_q(scopy, 256, 352)
-        round_q(vcopy, 352, 512)
-        shift(0)
-        weights(0)
-        quantise_q(256, 512)
-        for u in range(4, 8):
+        round_q(vcopy, 1)
+        round_q(scopy, 2)
+        round_q(scopy, 3)
+        quantise_q(2)
+        quantise_q(1)
+        for u in range(2, 6):
             scores(u)
-        for u in range(1, 8):
-            shift(u)
-            weights(u)
-        round_y(0, 256)
-        weights_bf(384, 512)
+        weights(0)
+        store_weights(0, 0, 2)
+        weights(1)
+        store_weights(0, 2, 4)
+        quantise_q(3)
+        scores(6)
+        scores(7)
+        weights(2)
+        weights(3)
+        store_weights(1, 0, 2)
+        weights(4)
+        weights(5)
+        store_weights(1, 2, 4)
+        weights(6)
+        weights(7)
+        store_weights(2, 0, 4)
+        nc.scalar.activation(woven(y_bf[:, 384:512, :]), planar(shifted[2][:]), EXP)
+        round_y(0, 128)
+        round_y(128, 256)
+        quantise_y(0, 128)
         round_y(256, 384)
-        quantise_y(0, 256)
-        store_words(0, HALF)
+        quantise_y(128, 256)
         quantise_y(256, 384)
         quantise_y(384, 512)
-        store_words(HALF, NQ)
+        store_words(0, NQ)
         store_scales(nc.scalar, 0)
         store_scales(nc.sync, 1)
         store_scales(nc.scalar, 2)

@@ -20,6 +20,7 @@ PACK = 4
 N, T, D, NQ = 512, 2048, 512, 512
 HALF = NQ // 2
 CH = 128
+FIRST = 384
 FLOPS = 2 * N * D * NQ
 
 
@@ -48,7 +49,7 @@ def tile_attend_plw_soft_kernel(tc, qT, k_words, k_scales, ls, offs, out_0, out_
 
         offsets = keep.tile([P, N // 16], U16, name="offsets")
         pool_words = sbuf([P, T], U32, "pool_words")
-        pool_scales = sbuf([P, T], U8, "pool_scales", "window")
+        pool_scales = sbuf([P, T], U8, "pool_scales")
         ls_cols = keep.tile([P, PACK], F32, name="ls_cols")
         ident = keep.tile([P, P], F32, name="ident")
         ls_bank = psum.tile([P, PACK, P], F32, name="ls_bank", tag="turned")
@@ -56,26 +57,23 @@ def tile_attend_plw_soft_kernel(tc, qT, k_words, k_scales, ls, offs, out_0, out_
         got_scales = sbuf([P, N], U8, "got_scales")
         k_plane = sbuf([P, N], U8, "k_plane")
         k_codes = sbuf([P, N], U32, "k_codes")
-        pieces = [(0, 128), (128, 384), (384, 512)]
-        q_raw = [sbuf([P, PACK, b - a], F32, "q_raw%d" % i, "raw%d" % i) for i, (a, b) in enumerate(pieces)]
+        pieces = [(0, 1), (1, 3), (3, 4)]
+        q_raw = [sbuf([P, PACK, (b - a) * CH], F32, "q_raw%d" % i, "raw%d" % i) for i, (a, b) in enumerate(pieces)]
         q_bf = [sbuf([P, CH, PACK], BF16, "q_bf%d" % c, "stage%d" % c) for c in range(chunks)]
-        q_codes = [sbuf([P, b - a], U32, "q_codes%d" % i, "window" if i == 0 else "") for i, (a, b) in enumerate(pieces)]
-        q_plane = [sbuf([P, b - a], U8, "q_plane%d" % i) for i, (a, b) in enumerate(pieces)]
-        shifted = [sbuf([P, PACK, b - a], F32, "shifted%d" % i, ("stage1", "", "stage3")[i]) for i, (a, b) in enumerate(pieces)]
+        q_codes = [sbuf([P, CH], U32, "q_codes%d" % c) for c in range(chunks)]
+        q_plane = [sbuf([P, CH], U8, "q_plane%d" % c) for c in range(chunks)]
+        shifted = [sbuf([P, PACK, CH], F32, "shifted%d" % c, "stage1" if c == 0 else "") for c in range(chunks)]
         y = sbuf([P, PACK, NQ], F32, "y", "raw2")
         y_bf = sbuf([P, NQ, PACK], BF16, "y_bf")
         y_codes = sbuf([P, NQ], U32, "y_codes")
         y_plane = sbuf([P, NQ], U8, "y_plane")
-        parts = [(0, 0, 2), (0, 2, 4), (1, 0, 1), (1, 1, 2), (1, 2, 3), (1, 3, 4), (2, 0, 2), (2, 2, 4)]
         banks = [
-            psum.tile([P, r1 - r0, pieces[i][1] - pieces[i][0]], F32, name="bank%d" % u, tag="turned" if u == len(parts) - 1 else "")
-            for u, (i, r0, r1) in enumerate(parts)
+            psum.tile([P, 2, CH], F32, name="bank%d" % u, tag="turned" if u == 2 * chunks - 1 else "")
+            for u in range(2 * chunks)
         ]
 
-        def piece_of(c):
-            i = max(i for i, piece in enumerate(pieces) if piece[0] <= c * CH)
-            a = c * CH - pieces[i][0]
-            return i, slice(a, a + CH)
+        def cols(c, end=None):
+            return slice(c * CH, (c + 1 if end is None else end) * CH)
 
         def load_scales(queue, quad):
             queue.dma_start(
@@ -84,60 +82,55 @@ def tile_attend_plw_soft_kernel(tc, qT, k_words, k_scales, ls, offs, out_0, out_
             )
 
         def load_q(i):
-            nc.sync.dma_start(q_raw[i][:], q_rows[:, :, pieces[i][0] : pieces[i][1]])
+            nc.sync.dma_start(q_raw[i][:], q_rows[:, :, cols(*pieces[i])])
 
         def round_q(copy, c):
-            i, cols = piece_of(c)
-            copy(woven(q_bf[c][:]), planar(q_raw[i][:, :, cols]))
+            i = max(i for i, piece in enumerate(pieces) if piece[0] <= c)
+            copy(woven(q_bf[c][:]), planar(q_raw[i][:, :, cols(c - pieces[i][0])]))
 
         def quantise_q(c):
-            i, cols = piece_of(c)
             nc.vector.quantize_mx(
-                out=q_codes[i][:, cols].bitcast(FP8X4),
-                scales=q_plane[i][:, cols],
+                out=q_codes[c][:].bitcast(FP8X4),
+                scales=q_plane[c][:],
                 in_=q_bf[c][:].rearrange("p q j -> p (q j)"),
             )
 
-        def scores(u):
-            i, r0, r1 = parts[u]
-            for r in range(r0, r1):
+        def scores(c):
+            for r in range(PACK):
                 nc.tensor.matmul_mx(
-                    out=banks[u][:, r - r0, :],
+                    out=banks[2 * c + r // 2][:, r % 2, :],
                     lhsT=k_codes[:, r * P : (r + 1) * P].bitcast(FP8X4),
                     lhsT_scale=k_plane[:, r * P : (r + 1) * P],
-                    rhs=q_codes[i][:].bitcast(FP8X4),
-                    rhs_scale=q_plane[i][:],
+                    rhs=q_codes[c][:].bitcast(FP8X4),
+                    rhs_scale=q_plane[c][:],
                     start=True,
                     stop=True,
                 )
 
-        def weights(u):
-            i, r0, r1 = parts[u]
-            a, b = pieces[i]
+        def weights(c, r):
             nc.vector.tensor_tensor(
-                shifted[i][:, r0:r1, :],
-                banks[u][:],
-                ls_rows[:, a:b].unsqueeze(1).to_broadcast([P, r1 - r0, b - a]),
+                shifted[c][:, r : r + 2, :],
+                banks[2 * c + r // 2][:],
+                ls_rows[:, cols(c)].unsqueeze(1).to_broadcast([P, 2, CH]),
                 SUB,
             )
-            nc.scalar.activation(y[:, r0:r1, a:b], shifted[i][:, r0:r1, :], EXP)
+            nc.scalar.activation(y[:, r : r + 2, cols(c)], shifted[c][:, r : r + 2, :], EXP)
 
-        def store_weights(i, r0, r1):
-            a, b = pieces[i]
-            nc.sync.dma_start(y_rows[:, r0:r1, a:b], y[:, r0:r1, a:b])
+        def store_weights(span, r0, r1):
+            nc.sync.dma_start(y_rows[:, r0:r1, span], y[:, r0:r1, span])
 
-        def round_y(a, b):
-            nc.vector.tensor_copy(woven(y_bf[:, a:b, :]), planar(y[:, :, a:b]))
+        def round_y(span):
+            nc.vector.tensor_copy(woven(y_bf[:, span, :]), planar(y[:, :, span]))
 
-        def quantise_y(a, b):
+        def quantise_y(span):
             nc.vector.quantize_mx(
-                out=y_codes[:, a:b].bitcast(FP8X4),
-                scales=y_plane[:, a:b],
-                in_=y_bf[:, a:b, :].rearrange("p q u -> p (q u)"),
+                out=y_codes[:, span].bitcast(FP8X4),
+                scales=y_plane[:, span],
+                in_=y_bf[:, span, :].rearrange("p q u -> p (q u)"),
             )
 
-        def store_words(a, b):
-            nc.sync.dma_start(y_words[:, a:b], y_codes[:, a:b].bitcast(I32))
+        def store_words(span):
+            nc.sync.dma_start(y_words[:, span], y_codes[:, span].bitcast(I32))
 
         def store_scales(queue, quad):
             queue.dma_start(
@@ -164,56 +157,53 @@ def tile_attend_plw_soft_kernel(tc, qT, k_words, k_scales, ls, offs, out_0, out_
         scopy = nc.scalar.copy
 
         nc.vector.memset(pool_scales[:].bitcast(I32), 0)
-        load_q(0)
+        nc.sync.dma_start(pool_words[:, 0:FIRST].bitcast(I32), k_rows[:, 0:FIRST])
         nc.sync.dma_start(offsets[:], offs)
-        nc.sync.dma_start(ls_cols[:], ls[0, 0].rearrange("(p j) -> p j", j=PACK))
+        nc.scalar.dma_start(ls_cols[:], ls[0, 0].rearrange("(p j) -> p j", j=PACK))
         for quad in range(4):
             load_scales(nc.scalar if quad % 2 else nc.sync, quad)
-        nc.sync.dma_start(pool_words[:].bitcast(I32), k_rows)
-        for i in range(1, len(pieces)):
+        nc.sync.dma_start(pool_words[:, FIRST:T].bitcast(I32), k_rows[:, FIRST:T])
+        for i in range(len(pieces)):
             load_q(i)
         spread_ls()
 
-        round_q(scopy, 0)
         vcopy(got_scales[:], pool_scales[:].indirect(offsets[:]))
-        quantise_q(0)
         vcopy(k_plane[:].rearrange("p (r s) -> p r s", r=PACK), got_scales[:].rearrange("p (s r) -> p r s", r=PACK))
         vcopy(k_codes[:].rearrange("p (r s) -> p s r", r=PACK), pool_words[:].indirect(offsets[:]))
 
+        round_q(scopy, 0)
+        quantise_q(0)
         scores(0)
-        scores(1)
         round_q(vcopy, 1)
         round_q(scopy, 2)
         round_q(scopy, 3)
-        quantise_q(2)
         quantise_q(1)
-        for u in range(2, 6):
-            scores(u)
-        weights(0)
-        store_weights(0, 0, 2)
-        weights(1)
-        store_weights(0, 2, 4)
+        scores(1)
+        weights(0, 0)
+        store_weights(cols(0), 0, 2)
+        quantise_q(2)
+        scores(2)
+        weights(0, 2)
+        store_weights(cols(0), 2, 4)
         quantise_q(3)
-        scores(6)
-        scores(7)
-        weights(2)
-        weights(3)
-        store_weights(1, 0, 2)
-        weights(4)
-        weights(5)
-        store_weights(1, 2, 4)
-        weights(6)
-        weights(7)
-        store_weights(2, 0, 4)
-        nc.scalar.activation(woven(y_bf[:, 384:512, :]), planar(shifted[2][:]), EXP)
-        round_y(0, 128)
-        round_y(128, 256)
-        quantise_y(0, 128)
-        round_y(256, 384)
-        quantise_y(128, 256)
-        quantise_y(256, 384)
-        quantise_y(384, 512)
-        store_words(0, NQ)
+        scores(3)
+        for c in range(1, chunks):
+            for r in (0, 2):
+                weights(c, r)
+                if c < 2:
+                    store_weights(cols(c), r, r + 2)
+            if c >= 2:
+                store_weights(cols(c), 0, PACK)
+        nc.scalar.activation(woven(y_bf[:, cols(3), :]), planar(shifted[3][:]), EXP)
+        round_y(cols(0))
+        round_y(cols(1))
+        quantise_y(cols(0))
+        round_y(cols(2))
+        quantise_y(cols(1))
+        quantise_y(cols(2))
+        store_words(cols(0, 3))
+        quantise_y(cols(3))
+        store_words(cols(3))
         store_scales(nc.scalar, 0)
         store_scales(nc.sync, 1)
         store_scales(nc.scalar, 2)

@@ -75,11 +75,8 @@ def tile_attend_plw_soft_kernel(tc, qT, k_words, k_scales, ls, offs, out_0, out_
         def cols(c, end=None):
             return slice(c * CH, (c + 1 if end is None else end) * CH)
 
-        def load_scales(queue, quad):
-            queue.dma_start(
-                pool_scales[32 * quad : 32 * quad + 4, :].bitcast(I32),
-                k_scales[0, 4 * quad : 4 * quad + 4, :].bitcast(I32),
-            )
+        def load_scales(queue, j):
+            queue.dma_start(pool_scales[j:P:32, :].bitcast(I32), k_scales[0, j:16:4, :].bitcast(I32))
 
         def load_q(i):
             nc.sync.dma_start(q_raw[i][:], q_rows[:, :, cols(*pieces[i])])
@@ -132,11 +129,8 @@ def tile_attend_plw_soft_kernel(tc, qT, k_words, k_scales, ls, offs, out_0, out_
         def store_words(span):
             nc.sync.dma_start(y_words[:, span], y_codes[:, span].bitcast(I32))
 
-        def store_scales(queue, quad):
-            queue.dma_start(
-                out_2[0, 4 * quad : 4 * quad + 4, :].bitcast(I32),
-                y_plane[32 * quad : 32 * quad + 4, :].bitcast(I32),
-            )
+        def store_scales(queue, j):
+            queue.dma_start(out_2[0, j:16:4, :].bitcast(I32), y_plane[j:P:32, :].bitcast(I32))
 
         def spread_ls():
             ones = keep.tile([P, 32], F32, name="ones")
@@ -160,8 +154,8 @@ def tile_attend_plw_soft_kernel(tc, qT, k_words, k_scales, ls, offs, out_0, out_
         nc.sync.dma_start(pool_words[:, 0:FIRST].bitcast(I32), k_rows[:, 0:FIRST])
         nc.sync.dma_start(offsets[:], offs)
         nc.scalar.dma_start(ls_cols[:], ls[0, 0].rearrange("(p j) -> p j", j=PACK))
-        for quad in range(4):
-            load_scales(nc.scalar if quad % 2 else nc.sync, quad)
+        for j in range(4):
+            load_scales(nc.scalar if j % 2 else nc.sync, j)
         nc.sync.dma_start(pool_words[:, FIRST:T].bitcast(I32), k_rows[:, FIRST:T])
         for i in range(len(pieces)):
             load_q(i)

@@ -36,6 +36,7 @@ def tile_attend_plw_soft_kernel(tc, qT, k_words, k_scales, ls, offs, out_0, out_
     nc = tc.nc
     with ExitStack() as ctx:
         keep = ctx.enter_context(tc.tile_pool(name="keep", bufs=1))
+        shared = ctx.enter_context(tc.tile_pool(name="shared", bufs=1))
         psum = ctx.enter_context(tc.psum_pool(name="psum", bufs=1))
 
         q_rows = qT[0].rearrange("(p j) q -> p j q", j=PACK)
@@ -57,13 +58,23 @@ def tile_attend_plw_soft_kernel(tc, qT, k_words, k_scales, ls, offs, out_0, out_
         got_scales = sbuf([P, N], U8, "got_scales")
         k_plane = sbuf([P, N], U8, "k_plane")
         k_codes = sbuf([P, N], U32, "k_codes")
-        pieces = [(0, 1), (1, 3), (3, 4)]
-        q_raw = [sbuf([P, PACK, (b - a) * CH], F32, "q_raw%d" % i, "raw%d" % i) for i, (a, b) in enumerate(pieces)]
+        pieces = [(0, 1), (1, 2), (2, 3), (3, 4)]
+        q_raw = [sbuf([P, PACK, (b - a) * CH], F32, "q_raw%d" % i, "raw%d" % i) for i, (a, b) in enumerate(pieces[:3])]
+        q_raw.append(shared.tile([P, PACK, CH], F32, name="q_raw3", offset=960))
         q_bf = [sbuf([P, CH, PACK], BF16, "q_bf%d" % c, "stage%d" % c) for c in range(chunks)]
         q_codes = [sbuf([P, CH], U32, "q_codes%d" % c) for c in range(chunks)]
         q_plane = [sbuf([P, CH], U8, "q_plane%d" % c) for c in range(chunks)]
-        shifted = [sbuf([P, PACK, CH], F32, "shifted%d" % c, "stage1" if c == 0 else "") for c in range(chunks)]
-        y = sbuf([P, PACK, NQ], F32, "y", "raw2")
+        over = {(0, 0): "raw1", (0, 2): "raw2", (2, 0): "raw1", (2, 2): "raw2"}
+        shifted = {
+            (c, r): sbuf([P, 2, CH], F32, "shifted%d_%d" % (c, r), over.get((c, r), ""))
+            for c in range(chunks - 1)
+            for r in (0, 2)
+            if c != 1
+        }
+        shifted.update({(1, 0): shared.tile([P, 2, CH], F32, name="shifted1_0", offset=0)})
+        shifted.update({(1, 2): shared.tile([P, 2, CH], F32, name="shifted1_2", offset=1024)})
+        last = sbuf([P, PACK, CH], F32, "last")
+        y = shared.tile([P, PACK, NQ], F32, name="y", offset=2048)
         y_bf = sbuf([P, NQ, PACK], BF16, "y_bf")
         y_codes = sbuf([P, NQ], U32, "y_codes")
         y_plane = sbuf([P, NQ], U8, "y_plane")
@@ -81,9 +92,8 @@ def tile_attend_plw_soft_kernel(tc, qT, k_words, k_scales, ls, offs, out_0, out_
         def load_q(i):
             nc.sync.dma_start(q_raw[i][:], q_rows[:, :, cols(*pieces[i])])
 
-        def round_q(copy, c):
-            i = max(i for i, piece in enumerate(pieces) if piece[0] <= c)
-            copy(woven(q_bf[c][:]), planar(q_raw[i][:, :, cols(c - pieces[i][0])]))
+        def round_q(copy, c, span=slice(0, CH)):
+            copy(woven(q_bf[c][:, span, :]), planar(q_raw[c][:, :, span]))
 
         def quantise_q(c):
             nc.vector.quantize_mx(
@@ -105,19 +115,23 @@ def tile_attend_plw_soft_kernel(tc, qT, k_words, k_scales, ls, offs, out_0, out_
                 )
 
         def weights(c, r):
+            part = last[:, r : r + 2, :] if c == chunks - 1 else shifted[c, r][:]
             nc.vector.tensor_tensor(
-                shifted[c][:, r : r + 2, :],
+                part,
                 banks[2 * c + r // 2][:],
                 ls_rows[:, cols(c)].unsqueeze(1).to_broadcast([P, 2, CH]),
                 SUB,
             )
-            nc.scalar.activation(y[:, r : r + 2, cols(c)], shifted[c][:, r : r + 2, :], EXP)
+            nc.scalar.activation(y[:, r : r + 2, cols(c)], part, EXP)
 
         def store_weights(span, r0, r1):
             nc.sync.dma_start(y_rows[:, r0:r1, span], y[:, r0:r1, span])
 
-        def round_y(span):
-            nc.vector.tensor_copy(woven(y_bf[:, span, :]), planar(y[:, :, span]))
+        def round_y(copy, span):
+            copy(woven(y_bf[:, span, :]), planar(y[:, :, span]))
+
+        def round_y_aside(span):
+            nc.gpsimd.tensor_scalar(y_bf[:, span, :], y[:, :, span].rearrange("p r q -> p q r"), 1.0, 0.0, MULT, ADD)
 
         def quantise_y(span):
             nc.vector.quantize_mx(
@@ -168,8 +182,9 @@ def tile_attend_plw_soft_kernel(tc, qT, k_words, k_scales, ls, offs, out_0, out_
         round_q(scopy, 0)
         quantise_q(0)
         scores(0)
-        round_q(vcopy, 1)
-        round_q(scopy, 2)
+        round_q(scopy, 1)
+        round_q(vcopy, 2, slice(0, 64))
+        round_q(scopy, 2, slice(64, CH))
         round_q(scopy, 3)
         quantise_q(1)
         scores(1)
@@ -181,20 +196,20 @@ def tile_attend_plw_soft_kernel(tc, qT, k_words, k_scales, ls, offs, out_0, out_
         store_weights(cols(0), 2, 4)
         quantise_q(3)
         scores(3)
+        round_y_aside(cols(0))
         for c in range(1, chunks):
             for r in (0, 2):
                 weights(c, r)
+                if c == 1 and r == 2:
+                    round_y_aside(slice(CH, CH + 64))
                 if c < 2:
                     store_weights(cols(c), r, r + 2)
             if c >= 2:
                 store_weights(cols(c), 0, PACK)
-        nc.scalar.activation(woven(y_bf[:, cols(3), :]), planar(shifted[3][:]), EXP)
-        round_y(cols(0))
-        round_y(cols(1))
+        nc.scalar.activation(woven(y_bf[:, cols(3), :]), planar(last[:]), EXP)
+        round_y(vcopy, slice(CH + 64, 3 * CH))
         quantise_y(cols(0))
-        round_y(cols(2))
-        quantise_y(cols(1))
-        quantise_y(cols(2))
+        quantise_y(cols(1, 3))
         store_words(cols(0, 3))
         quantise_y(cols(3))
         store_words(cols(3))

@@ -20,7 +20,7 @@ PACK = 4
 N, T, D, NQ = 512, 2048, 512, 512
 HALF = NQ // 2
 CH = 128
-FIRST = 384
+FIRST = 576
 FLOPS = 2 * N * D * NQ
 
 
@@ -55,26 +55,18 @@ def tile_attend_plw_soft_kernel(tc, qT, k_words, k_scales, ls, offs, out_0, out_
         ident = keep.tile([P, P], F32, name="ident")
         ls_bank = psum.tile([P, PACK, P], F32, name="ls_bank", tag="turned")
         ls_rows = sbuf([P, NQ], F32, "ls_rows")
-        got_scales = sbuf([P, N], U8, "got_scales")
+        got_scales = [sbuf([P, N // 2], U8, "got_scales%d" % h) for h in range(2)]
         k_plane = sbuf([P, N], U8, "k_plane")
         k_codes = sbuf([P, N], U32, "k_codes")
         pieces = [(0, 1), (1, 2), (2, 3), (3, 4)]
         q_raw = [sbuf([P, PACK, (b - a) * CH], F32, "q_raw%d" % i, "raw%d" % i) for i, (a, b) in enumerate(pieces[:3])]
-        q_raw.append(shared.tile([P, PACK, CH], F32, name="q_raw3", offset=960))
+        q_raw.append(shared.tile([P, PACK, CH], F32, name="q_raw3", offset=5120))
         q_bf = [sbuf([P, CH, PACK], BF16, "q_bf%d" % c, "stage%d" % c) for c in range(chunks)]
         q_codes = [sbuf([P, CH], U32, "q_codes%d" % c) for c in range(chunks)]
-        q_plane = [sbuf([P, CH], U8, "q_plane%d" % c) for c in range(chunks)]
-        over = {(0, 0): "raw1", (0, 2): "raw2", (2, 0): "raw1", (2, 2): "raw2"}
-        shifted = {
-            (c, r): sbuf([P, 2, CH], F32, "shifted%d_%d" % (c, r), over.get((c, r), ""))
-            for c in range(chunks - 1)
-            for r in (0, 2)
-            if c != 1
-        }
-        shifted.update({(1, 0): shared.tile([P, 2, CH], F32, name="shifted1_0", offset=0)})
-        shifted.update({(1, 2): shared.tile([P, 2, CH], F32, name="shifted1_2", offset=1024)})
-        last = sbuf([P, PACK, CH], F32, "last")
-        y = shared.tile([P, PACK, NQ], F32, name="y", offset=2048)
+        q_plane = [sbuf([P, CH], U8, "q_plane%d" % c, "plane0" if c in (0, 3) else "") for c in range(chunks)]
+        early = [sbuf([P, 2, CH], F32, "early%d" % h, "" if h else "raw1") for h in range(2)]
+        late = shared.tile([P, (chunks - 1) * PACK, CH], F32, name="late", offset=0)
+        y = shared.tile([P, PACK, NQ], F32, name="y", offset=6144)
         y_bf = sbuf([P, NQ, PACK], BF16, "y_bf")
         y_codes = sbuf([P, NQ], U32, "y_codes")
         y_plane = sbuf([P, NQ], U8, "y_plane")
@@ -115,7 +107,7 @@ def tile_attend_plw_soft_kernel(tc, qT, k_words, k_scales, ls, offs, out_0, out_
                 )
 
         def weights(c, r):
-            part = last[:, r : r + 2, :] if c == chunks - 1 else shifted[c, r][:]
+            part = early[r // 2][:] if c == 0 else late[:, (c - 1) * PACK + r : (c - 1) * PACK + r + 2, :]
             nc.vector.tensor_tensor(
                 part,
                 banks[2 * c + r // 2][:],
@@ -129,9 +121,6 @@ def tile_attend_plw_soft_kernel(tc, qT, k_words, k_scales, ls, offs, out_0, out_
 
         def round_y(copy, span):
             copy(woven(y_bf[:, span, :]), planar(y[:, :, span]))
-
-        def round_y_aside(span):
-            nc.gpsimd.tensor_scalar(y_bf[:, span, :], y[:, :, span].rearrange("p r q -> p q r"), 1.0, 0.0, MULT, ADD)
 
         def quantise_y(span):
             nc.vector.quantize_mx(
@@ -175,8 +164,13 @@ def tile_attend_plw_soft_kernel(tc, qT, k_words, k_scales, ls, offs, out_0, out_
             load_q(i)
         spread_ls()
 
-        vcopy(got_scales[:], pool_scales[:].indirect(offsets[:]))
-        vcopy(k_plane[:].rearrange("p (r s) -> p r s", r=PACK), got_scales[:].rearrange("p (s r) -> p r s", r=PACK))
+        for h in range(2):
+            vcopy(got_scales[h][:], pool_scales[:].indirect(offsets[:, 16 * h : 16 * h + 16]))
+        for h in range(2):
+            vcopy(
+                k_plane[:].rearrange("p (r s) -> p r s", r=PACK)[:, :, 64 * h : 64 * h + 64],
+                got_scales[h][:].rearrange("p (s r) -> p r s", r=PACK),
+            )
         vcopy(k_codes[:].rearrange("p (r s) -> p s r", r=PACK), pool_words[:].indirect(offsets[:]))
 
         round_q(scopy, 0)
@@ -188,28 +182,26 @@ def tile_attend_plw_soft_kernel(tc, qT, k_words, k_scales, ls, offs, out_0, out_
         round_q(scopy, 3)
         quantise_q(1)
         scores(1)
-        weights(0, 0)
-        store_weights(cols(0), 0, 2)
         quantise_q(2)
         scores(2)
+        weights(0, 0)
+        store_weights(cols(0), 0, 2)
         weights(0, 2)
         store_weights(cols(0), 2, 4)
         quantise_q(3)
         scores(3)
-        round_y_aside(cols(0))
         for c in range(1, chunks):
             for r in (0, 2):
                 weights(c, r)
-                if c == 1 and r == 2:
-                    round_y_aside(slice(CH, CH + 64))
                 if c < 2:
                     store_weights(cols(c), r, r + 2)
             if c >= 2:
                 store_weights(cols(c), 0, PACK)
-        nc.scalar.activation(woven(y_bf[:, cols(3), :]), planar(last[:]), EXP)
-        round_y(vcopy, slice(CH + 64, 3 * CH))
-        quantise_y(cols(0))
-        quantise_y(cols(1, 3))
+        nc.scalar.activation(woven(y_bf[:, cols(3), :]), planar(late[:, 2 * PACK : 3 * PACK, :]), EXP)
+        round_y(vcopy, cols(0, 2))
+        round_y(vcopy, cols(2))
+        quantise_y(cols(0, 2))
+        quantise_y(cols(2))
         store_words(cols(0, 3))
         quantise_y(cols(3))
         store_words(cols(3))

@@ -58,13 +58,13 @@ def tile_attend_plw_soft_kernel(tc, qT, k_words, k_scales, ls, offs, out_0, out_
         got_scales = [sbuf([P, N // 2], U8, "got_scales%d" % h) for h in range(2)]
         k_plane = sbuf([P, N], U8, "k_plane")
         k_codes = sbuf([P, N], U32, "k_codes")
-        pieces = [(0, 1), (1, 2), (2, 3), (3, 4)]
-        q_raw = [sbuf([P, PACK, (b - a) * CH], F32, "q_raw%d" % i, "raw%d" % i) for i, (a, b) in enumerate(pieces[:3])]
+        pieces = [(0, 1), (1, 3), (3, 4)]
+        q_raw = [sbuf([P, PACK, (b - a) * CH], F32, "q_raw%d" % i, "raw%d" % i) for i, (a, b) in enumerate(pieces[:2])]
         q_raw.append(shared.tile([P, PACK, CH], F32, name="q_raw3", offset=5120))
         q_bf = [sbuf([P, CH, PACK], BF16, "q_bf%d" % c, "stage%d" % c) for c in range(chunks)]
         q_codes = [sbuf([P, CH], U32, "q_codes%d" % c) for c in range(chunks)]
         q_plane = [sbuf([P, CH], U8, "q_plane%d" % c, "plane0" if c in (0, 3) else "") for c in range(chunks)]
-        early = [sbuf([P, 2, CH], F32, "early%d" % h, "" if h else "raw1") for h in range(2)]
+        early = sbuf([P, PACK, CH], F32, "early", "raw1")
         late = shared.tile([P, (chunks - 1) * PACK, CH], F32, name="late", offset=0)
         y = shared.tile([P, PACK, NQ], F32, name="y", offset=6144)
         y_bf = sbuf([P, NQ, PACK], BF16, "y_bf")
@@ -84,8 +84,9 @@ def tile_attend_plw_soft_kernel(tc, qT, k_words, k_scales, ls, offs, out_0, out_
         def load_q(i):
             nc.sync.dma_start(q_raw[i][:], q_rows[:, :, cols(*pieces[i])])
 
-        def round_q(copy, c, span=slice(0, CH)):
-            copy(woven(q_bf[c][:, span, :]), planar(q_raw[c][:, :, span]))
+        def round_q(copy, c):
+            i = max(i for i, piece in enumerate(pieces) if piece[0] <= c)
+            copy(woven(q_bf[c][:]), planar(q_raw[i][:, :, cols(c - pieces[i][0])]))
 
         def quantise_q(c):
             nc.vector.quantize_mx(
@@ -107,7 +108,7 @@ def tile_attend_plw_soft_kernel(tc, qT, k_words, k_scales, ls, offs, out_0, out_
                 )
 
         def weights(c, r):
-            part = early[r // 2][:] if c == 0 else late[:, (c - 1) * PACK + r : (c - 1) * PACK + r + 2, :]
+            part = early[:, r : r + 2, :] if c == 0 else late[:, (c - 1) * PACK + r : (c - 1) * PACK + r + 2, :]
             nc.vector.tensor_tensor(
                 part,
                 banks[2 * c + r // 2][:],
@@ -176,9 +177,8 @@ def tile_attend_plw_soft_kernel(tc, qT, k_words, k_scales, ls, offs, out_0, out_
         round_q(scopy, 0)
         quantise_q(0)
         scores(0)
-        round_q(scopy, 1)
-        round_q(vcopy, 2, slice(0, 64))
-        round_q(scopy, 2, slice(64, CH))
+        round_q(vcopy, 1)
+        round_q(scopy, 2)
         round_q(scopy, 3)
         quantise_q(1)
         scores(1)

@@ -84,9 +84,10 @@ def tile_attend_plw_soft_kernel(tc, qT, k_words, k_scales, ls, offs, out_0, out_
         def load_q(i):
             nc.sync.dma_start(q_raw[i][:], q_rows[:, :, cols(*pieces[i])])
 
-        def round_q(copy, c):
+        def round_q(copy, c, a=0, b=CH):
             i = max(i for i, piece in enumerate(pieces) if piece[0] <= c)
-            copy(woven(q_bf[c][:]), planar(q_raw[i][:, :, cols(c - pieces[i][0])]))
+            first = (c - pieces[i][0]) * CH
+            copy(woven(q_bf[c][:, a:b, :]), planar(q_raw[i][:, :, first + a : first + b]))
 
         def quantise_q(c):
             nc.vector.quantize_mx(
@@ -122,6 +123,9 @@ def tile_attend_plw_soft_kernel(tc, qT, k_words, k_scales, ls, offs, out_0, out_
 
         def round_y(copy, span):
             copy(woven(y_bf[:, span, :]), planar(y[:, :, span]))
+
+        def round_y_aside(span):
+            nc.gpsimd.tensor_scalar(y_bf[:, span, :], y[:, :, span].rearrange("p r q -> p q r"), 1.0, 0.0, MULT, ADD)
 
         def quantise_y(span):
             nc.vector.quantize_mx(
@@ -177,8 +181,9 @@ def tile_attend_plw_soft_kernel(tc, qT, k_words, k_scales, ls, offs, out_0, out_
         round_q(scopy, 0)
         quantise_q(0)
         scores(0)
-        round_q(vcopy, 1)
-        round_q(scopy, 2)
+        for c in (1, 2):
+            round_q(vcopy, c, 0, 80)
+            round_q(scopy, c, 80, CH)
         round_q(scopy, 3)
         quantise_q(1)
         scores(1)
@@ -190,6 +195,7 @@ def tile_attend_plw_soft_kernel(tc, qT, k_words, k_scales, ls, offs, out_0, out_
         store_weights(cols(0), 2, 4)
         quantise_q(3)
         scores(3)
+        round_y_aside(cols(0))
         for c in range(1, chunks):
             for r in (0, 2):
                 weights(c, r)
@@ -198,7 +204,7 @@ def tile_attend_plw_soft_kernel(tc, qT, k_words, k_scales, ls, offs, out_0, out_
             if c >= 2:
                 store_weights(cols(c), 0, PACK)
         nc.scalar.activation(woven(y_bf[:, cols(3), :]), planar(late[:, 2 * PACK : 3 * PACK, :]), EXP)
-        round_y(vcopy, cols(0, 2))
+        round_y(vcopy, cols(1))
         round_y(vcopy, cols(2))
         quantise_y(cols(0, 2))
         quantise_y(cols(2))

@@ -62,18 +62,19 @@ def tile_attend_plw_soft_kernel(tc, qT, k_words, k_scales, ls, offs, out_0, out_
         q_raw = [sbuf([P, PACK, (b - a) * CH], F32, "q_raw%d" % i, "raw%d" % i) for i, (a, b) in enumerate(pieces[:2])]
         q_raw.append(shared.tile([P, PACK, CH], F32, name="q_raw3", offset=5120))
         q_bf = [sbuf([P, CH, PACK], BF16, "q_bf%d" % c, "stage%d" % c) for c in range(chunks)]
-        q_codes = [sbuf([P, CH], U32, "q_codes%d" % c) for c in range(chunks)]
+        q_codes = [sbuf([P, CH], U32, "q_codes%d" % c, "codes3" if c == 3 else "") for c in range(chunks)]
         q_plane = [sbuf([P, CH], U8, "q_plane%d" % c, "plane0" if c in (0, 3) else "") for c in range(chunks)]
         early = sbuf([P, PACK, CH], F32, "early", "raw1")
         late = shared.tile([P, (chunks - 1) * PACK, CH], F32, name="late", offset=0)
         y = shared.tile([P, PACK, NQ], F32, name="y", offset=6144)
-        y_bf = sbuf([P, NQ, PACK], BF16, "y_bf")
+        y_bf = sbuf([P, NQ, PACK], BF16, "y_bf", "codes3")
         y_codes = sbuf([P, NQ], U32, "y_codes")
         y_plane = sbuf([P, NQ], U8, "y_plane")
         banks = [
-            psum.tile([P, 2, CH], F32, name="bank%d" % u, tag="turned" if u == 2 * chunks - 1 else "")
+            psum.tile([P, 2, CH], F32, name="bank%d" % u, tag={0: "first", 2 * chunks - 1: "turned"}.get(u, ""))
             for u in range(2 * chunks)
         ]
+        last_bank = psum.tile([P, CH], F32, name="last_bank", tag="first")
 
         def cols(c, end=None):
             return slice(c * CH, (c + 1 if end is None else end) * CH)
@@ -99,7 +100,7 @@ def tile_attend_plw_soft_kernel(tc, qT, k_words, k_scales, ls, offs, out_0, out_
         def scores(c):
             for r in range(PACK):
                 nc.tensor.matmul_mx(
-                    out=banks[2 * c + r // 2][:, r % 2, :],
+                    out=last_bank[:] if (c, r) == (3, 3) else banks[2 * c + r // 2][:, r % 2, :],
                     lhsT=k_codes[:, r * P : (r + 1) * P].bitcast(FP8X4),
                     lhsT_scale=k_plane[:, r * P : (r + 1) * P],
                     rhs=q_codes[c][:].bitcast(FP8X4),
@@ -118,14 +119,16 @@ def tile_attend_plw_soft_kernel(tc, qT, k_words, k_scales, ls, offs, out_0, out_
             )
             nc.scalar.activation(y[:, r : r + 2, cols(c)], part, EXP)
 
+        def one_place(r, bank):
+            part = late[:, 2 * PACK + r, :]
+            nc.vector.tensor_tensor(part, bank, ls_rows[:, cols(3)], SUB)
+            nc.scalar.activation(y[:, r, cols(3)], part, EXP)
+
         def store_weights(span, r0, r1):
             nc.sync.dma_start(y_rows[:, r0:r1, span], y[:, r0:r1, span])
 
         def round_y(copy, span):
             copy(woven(y_bf[:, span, :]), planar(y[:, :, span]))
-
-        def round_y_aside(span):
-            nc.gpsimd.tensor_scalar(y_bf[:, span, :], y[:, :, span].rearrange("p r q -> p q r"), 1.0, 0.0, MULT, ADD)
 
         def quantise_y(span):
             nc.vector.quantize_mx(
@@ -195,16 +198,19 @@ def tile_attend_plw_soft_kernel(tc, qT, k_words, k_scales, ls, offs, out_0, out_
         store_weights(cols(0), 2, 4)
         quantise_q(3)
         scores(3)
-        round_y_aside(cols(0))
         for c in range(1, chunks):
             for r in (0, 2):
-                weights(c, r)
+                if (c, r) == (3, 2):
+                    one_place(2, banks[7][:, 0, :])
+                    one_place(3, last_bank[:])
+                else:
+                    weights(c, r)
                 if c < 2:
                     store_weights(cols(c), r, r + 2)
             if c >= 2:
                 store_weights(cols(c), 0, PACK)
         nc.scalar.activation(woven(y_bf[:, cols(3), :]), planar(late[:, 2 * PACK : 3 * PACK, :]), EXP)
-        round_y(vcopy, cols(1))
+        round_y(vcopy, cols(0, 2))
         round_y(vcopy, cols(2))
         quantise_y(cols(0, 2))
         quantise_y(cols(2))

@@ -21,6 +21,7 @@ N, T, D, NQ = 512, 2048, 512, 512
 HALF = NQ // 2
 CH = 128
 FIRST = 576
+BURST = 256
 FLOPS = 2 * N * D * NQ
 
 
@@ -45,12 +46,12 @@ def tile_attend_plw_soft_kernel(tc, qT, k_words, k_scales, ls, offs, out_0, out_
         y_words = out_1[0].rearrange("p q u -> p (q u)").bitcast(I32)
         chunks = NQ // CH
 
-        def sbuf(shape, dtype, name, tag=""):
-            return keep.tile(shape, dtype, name=name, tag=tag, align_bytes=64)
+        def sbuf(shape, dtype, name, tag="", align=64):
+            return keep.tile(shape, dtype, name=name, tag=tag, align_bytes=align)
 
         offsets = keep.tile([P, N // 16], U16, name="offsets")
-        pool_words = sbuf([P, T], U32, "pool_words")
-        pool_scales = sbuf([P, T], U8, "pool_scales")
+        pool_words = sbuf([P, T], U32, "pool_words", "", BURST)
+        pool_scales = sbuf([P, T], U8, "pool_scales", "", BURST)
         ls_cols = keep.tile([P, PACK], F32, name="ls_cols")
         ident = keep.tile([P, P], F32, name="ident")
         ls_bank = psum.tile([P, PACK, P], F32, name="ls_bank", tag="turned")
@@ -59,17 +60,17 @@ def tile_attend_plw_soft_kernel(tc, qT, k_words, k_scales, ls, offs, out_0, out_
         k_plane = sbuf([P, N], U8, "k_plane")
         k_codes = sbuf([P, N], U32, "k_codes")
         pieces = [(0, 1), (1, 3), (3, 4)]
-        q_raw = [sbuf([P, PACK, (b - a) * CH], F32, "q_raw%d" % i, "raw%d" % i) for i, (a, b) in enumerate(pieces[:2])]
-        q_raw.append(shared.tile([P, PACK, CH], F32, name="q_raw3", offset=5120))
+        q_raw = [sbuf([P, PACK, (b - a) * CH], F32, "q_raw%d" % i, "raw%d" % i, BURST) for i, (a, b) in enumerate(pieces[:2])]
+        q_raw.append(shared.tile([P, PACK, CH], F32, name="q_raw3", offset=5120, align_bytes=BURST))
         q_bf = [sbuf([P, CH, PACK], BF16, "q_bf%d" % c, "stage%d" % c) for c in range(chunks)]
         q_codes = [sbuf([P, CH], U32, "q_codes%d" % c, "codes3" if c == 3 else "") for c in range(chunks)]
         q_plane = [sbuf([P, CH], U8, "q_plane%d" % c, "plane0" if c in (0, 3) else "") for c in range(chunks)]
-        early = sbuf([P, PACK, CH], F32, "early", "raw1")
-        late = shared.tile([P, (chunks - 1) * PACK, CH], F32, name="late", offset=0)
-        y = shared.tile([P, PACK, NQ], F32, name="y", offset=6144)
+        early = sbuf([P, PACK, CH], F32, "early", "raw1", BURST)
+        late = shared.tile([P, (chunks - 1) * PACK, CH], F32, name="late", offset=0, align_bytes=BURST)
+        y = shared.tile([P, PACK, NQ], F32, name="y", offset=6144, align_bytes=BURST)
         y_bf = sbuf([P, NQ, PACK], BF16, "y_bf", "codes3")
-        y_codes = sbuf([P, NQ], U32, "y_codes")
-        y_plane = sbuf([P, NQ], U8, "y_plane")
+        y_codes = sbuf([P, NQ], U32, "y_codes", "", BURST)
+        y_plane = sbuf([P, NQ], U8, "y_plane", "", BURST)
         banks = [
             psum.tile([P, 2, CH], F32, name="bank%d" % u, tag={0: "first", 2 * chunks - 1: "turned"}.get(u, ""))
             for u in range(2 * chunks)

@@ -56,7 +56,6 @@ def tile_attend_plw_soft_kernel(tc, qT, k_words, k_scales, ls, offs, out_0, out_
         ident = keep.tile([P, P], F32, name="ident")
         ls_bank = psum.tile([P, PACK, P], F32, name="ls_bank", tag="turned")
         ls_rows = sbuf([P, NQ], F32, "ls_rows")
-        got_scales = [sbuf([P, N // 2], U8, "got_scales%d" % h) for h in range(2)]
         k_plane = sbuf([P, N], U8, "k_plane")
         k_codes = sbuf([P, N], U32, "k_codes")
         pieces = [(0, 1), (1, 3), (3, 4)]
@@ -173,13 +172,7 @@ def tile_attend_plw_soft_kernel(tc, qT, k_words, k_scales, ls, offs, out_0, out_
             load_q(i)
         spread_ls()
 
-        for h in range(2):
-            vcopy(got_scales[h][:], pool_scales[:].indirect(offsets[:, 16 * h : 16 * h + 16]))
-        for h in range(2):
-            vcopy(
-                k_plane[:].rearrange("p (r s) -> p r s", r=PACK)[:, :, 64 * h : 64 * h + 64],
-                got_scales[h][:].rearrange("p (s r) -> p r s", r=PACK),
-            )
+        vcopy(k_plane[:].rearrange("p (r s) -> p s r", r=PACK), pool_scales[:].indirect(offsets[:]))
         vcopy(k_codes[:].rearrange("p (r s) -> p s r", r=PACK), pool_words[:].indirect(offsets[:]))
 
         round_q(scopy, 0)

@@ -18,11 +18,13 @@ EQUAL = mybir.AluOpType.is_equal
 P = 128
 PACK = 4
 N, T, D, NQ = 512, 2048, 512, 512
-HALF = NQ // 2
 CH = 128
+CHUNKS = NQ // CH
 FIRST = 576
+LAST = 64
 BURST = 256
 FLOPS = 2 * N * D * NQ
+WIDTH = {F32: 4, U32: 4, BF16: 2, U8: 1}
 
 
 def woven(dst):
@@ -33,51 +35,62 @@ def planar(src):
     return src.rearrange("p t (c i) -> p c t i", i=4)
 
 
+def cols(c, end=None):
+    return slice(c * CH, (c + 1 if end is None else end) * CH)
+
+
 def tile_attend_plw_soft_kernel(tc, qT, k_words, k_scales, ls, offs, out_0, out_1, out_2):
     nc = tc.nc
     with ExitStack() as ctx:
         keep = ctx.enter_context(tc.tile_pool(name="keep", bufs=1))
-        shared = ctx.enter_context(tc.tile_pool(name="shared", bufs=1))
+        placed = ctx.enter_context(tc.tile_pool(name="placed", bufs=1))
         psum = ctx.enter_context(tc.psum_pool(name="psum", bufs=1))
 
         q_rows = qT[0].rearrange("(p j) q -> p j q", j=PACK)
         k_rows = k_words[0].rearrange("p t r -> p (t r)").bitcast(I32)
         y_rows = out_0.rearrange("(p r) q -> p r q", r=PACK)
         y_words = out_1[0].rearrange("p q u -> p (q u)").bitcast(I32)
-        chunks = NQ // CH
 
-        def sbuf(shape, dtype, name, tag="", align=64):
-            return keep.tile(shape, dtype, name=name, tag=tag, align_bytes=align)
+        spot = {"free": 0}
+
+        def sbuf(shape, dtype, name, over="free", shift=0):
+            size = WIDTH[dtype]
+            for n in shape[1:]:
+                size = size * n
+            spot[name] = spot[over] + shift
+            if over == "free":
+                spot["free"] = spot["free"] + -(-size // BURST) * BURST
+            return placed.tile(shape, dtype, name=name, offset=spot[name], align_bytes=BURST)
+
+        vcopy = nc.vector.tensor_copy
+        scopy = nc.scalar.copy
 
         offsets = keep.tile([P, N // 16], U16, name="offsets")
-        pool_words = sbuf([P, T], U32, "pool_words", "", BURST)
-        pool_scales = sbuf([P, T], U8, "pool_scales", "", BURST)
         ls_cols = keep.tile([P, PACK], F32, name="ls_cols")
-        ident = keep.tile([P, P], F32, name="ident")
-        ls_bank = psum.tile([P, PACK, P], F32, name="ls_bank", tag="turned")
+        pool_words = sbuf([P, T], U32, "pool_words")
+        pool_scales = sbuf([P, T], U8, "pool_scales")
+        ident = sbuf([P, P], F32, "ident")
         ls_rows = sbuf([P, NQ], F32, "ls_rows")
         k_plane = sbuf([P, N], U8, "k_plane")
         k_codes = sbuf([P, N], U32, "k_codes")
+        late = sbuf([P, CHUNKS - 1, PACK, CH], F32, "late")
+        y = sbuf([P, PACK, NQ], F32, "y")
         pieces = [(0, 1), (1, 3), (3, 4)]
-        q_raw = [sbuf([P, PACK, (b - a) * CH], F32, "q_raw%d" % i, "raw%d" % i, BURST) for i, (a, b) in enumerate(pieces[:2])]
-        q_raw.append(shared.tile([P, PACK, CH], F32, name="q_raw3", offset=5120, align_bytes=BURST))
-        q_bf = [sbuf([P, CH, PACK], BF16, "q_bf%d" % c, "stage%d" % c) for c in range(chunks)]
-        q_codes = [sbuf([P, CH], U32, "q_codes%d" % c, "codes3" if c == 3 else "") for c in range(chunks)]
-        q_plane = [sbuf([P, CH], U8, "q_plane%d" % c, "plane0" if c in (0, 3) else "") for c in range(chunks)]
-        early = sbuf([P, PACK, CH], F32, "early", "raw1", BURST)
-        late = shared.tile([P, (chunks - 1) * PACK, CH], F32, name="late", offset=0, align_bytes=BURST)
-        y = shared.tile([P, PACK, NQ], F32, name="y", offset=6144, align_bytes=BURST)
-        y_bf = sbuf([P, NQ, PACK], BF16, "y_bf", "codes3")
-        y_codes = sbuf([P, NQ], U32, "y_codes", "", BURST)
-        y_plane = sbuf([P, NQ], U8, "y_plane", "", BURST)
+        q_raw = [sbuf([P, PACK, (b - a) * CH], F32, "q_raw%d" % i) for i, (a, b) in enumerate(pieces[:2])]
+        q_raw.append(sbuf([P, PACK, CH], F32, "q_raw2", "y", -1024))
+        q_bf = [sbuf([P, CH, PACK], BF16, "q_bf%d" % c) for c in range(CHUNKS)]
+        y_bf = sbuf([P, NQ, PACK], BF16, "y_bf")
+        y_plane = sbuf([P, NQ], U8, "y_plane")
+        q_codes = [sbuf([P, CH], U32, "q_codes%d" % c) for c in range(CHUNKS)]
+        q_plane = [sbuf([P, CH], U8, "q_plane%d" % c, "y_plane" if c in (0, 3) else "free") for c in range(CHUNKS)]
+        early = sbuf([P, PACK, CH], F32, "early", "q_raw1")
+        y_codes = sbuf([P, NQ], U32, "y_codes")
+        ls_bank = psum.tile([P, PACK, P], F32, name="ls_bank", tag="turned")
         banks = [
-            psum.tile([P, 2, CH], F32, name="bank%d" % u, tag={0: "first", 2 * chunks - 1: "turned"}.get(u, ""))
-            for u in range(2 * chunks)
+            psum.tile([P, 2, CH], F32, name="bank%d" % u, tag={0: "first", 2 * CHUNKS - 1: "turned"}.get(u, ""))
+            for u in range(2 * CHUNKS)
         ]
         last_bank = psum.tile([P, CH], F32, name="last_bank", tag="first")
-
-        def cols(c, end=None):
-            return slice(c * CH, (c + 1 if end is None else end) * CH)
 
         def load_scales(queue, j):
             queue.dma_start(pool_scales[j:P:32, :].bitcast(I32), k_scales[0, j:16:4, :].bitcast(I32))
@@ -110,7 +123,7 @@ def tile_attend_plw_soft_kernel(tc, qT, k_words, k_scales, ls, offs, out_0, out_
                 )
 
         def weights(c, r):
-            part = early[:, r : r + 2, :] if c == 0 else late[:, (c - 1) * PACK + r : (c - 1) * PACK + r + 2, :]
+            part = early[:, r : r + 2, :] if c == 0 else late[:, c - 1, r : r + 2, :]
             nc.vector.tensor_tensor(
                 part,
                 banks[2 * c + r // 2][:],
@@ -120,21 +133,27 @@ def tile_attend_plw_soft_kernel(tc, qT, k_words, k_scales, ls, offs, out_0, out_
             nc.scalar.activation(y[:, r : r + 2, cols(c)], part, EXP)
 
         def one_place(r, bank):
-            part = late[:, 2 * PACK + r, :]
+            part = late[:, 2, r, :]
             nc.vector.tensor_tensor(part, bank, ls_rows[:, cols(3)], SUB)
             nc.scalar.activation(y[:, r, cols(3)], part, EXP)
+
+        def rounded(span):
+            return y_bf[:, span, :]
+
+        def round_early(span):
+            nc.gpsimd.tensor_scalar(rounded(span), y[:, :, span].rearrange("p t q -> p q t"), 1.0, 0.0, MULT, ADD)
 
         def store_weights(span, r0, r1):
             nc.sync.dma_start(y_rows[:, r0:r1, span], y[:, r0:r1, span])
 
         def round_y(copy, span):
-            copy(woven(y_bf[:, span, :]), planar(y[:, :, span]))
+            copy(woven(rounded(span)), planar(y[:, :, span]))
 
         def quantise_y(span):
             nc.vector.quantize_mx(
                 out=y_codes[:, span].bitcast(FP8X4),
                 scales=y_plane[:, span],
-                in_=y_bf[:, span, :].rearrange("p q u -> p (q u)"),
+                in_=rounded(span).rearrange("p q u -> p (q u)"),
             )
 
         def store_words(span):
@@ -157,9 +176,6 @@ def tile_attend_plw_soft_kernel(tc, qT, k_words, k_scales, ls, offs, out_0, out_
             for j in range(PACK):
                 nc.tensor.transpose(ls_bank[:, j, :], ls_cols[:, j : j + 1].to_broadcast([P, P]), ident[:])
             nc.scalar.copy(ls_rows[:].rearrange("p (n j) -> p n j", j=PACK), ls_bank[:].rearrange("p j n -> p n j"))
-
-        vcopy = nc.vector.tensor_copy
-        scopy = nc.scalar.copy
 
         nc.vector.memset(pool_scales[:].bitcast(I32), 0)
         nc.sync.dma_start(pool_words[:, 0:FIRST].bitcast(I32), k_rows[:, 0:FIRST])
@@ -190,26 +206,30 @@ def tile_attend_plw_soft_kernel(tc, qT, k_words, k_scales, ls, offs, out_0, out_
         store_weights(cols(0), 0, 2)
         weights(0, 2)
         store_weights(cols(0), 2, 4)
+        round_early(cols(0))
         quantise_q(3)
         scores(3)
-        for c in range(1, chunks):
-            for r in (0, 2):
-                if (c, r) == (3, 2):
-                    one_place(2, banks[7][:, 0, :])
-                    one_place(3, last_bank[:])
-                else:
-                    weights(c, r)
-                if c < 2:
-                    store_weights(cols(c), r, r + 2)
-            if c >= 2:
-                store_weights(cols(c), 0, PACK)
-        nc.scalar.activation(woven(y_bf[:, cols(3), :]), planar(late[:, 2 * PACK : 3 * PACK, :]), EXP)
-        round_y(vcopy, cols(0, 2))
+        weights(1, 0)
+        store_weights(cols(1), 0, 2)
+        weights(1, 2)
+        store_weights(cols(1), 2, 4)
+        weights(2, 0)
+        weights(2, 2)
+        store_weights(cols(2), 0, PACK)
+        weights(3, 0)
+        one_place(2, banks[7][:, 0, :])
+        one_place(3, last_bank[:])
+        store_weights(cols(3), 0, PACK)
+        for a, b in ((0, CH - LAST), (CH - LAST, CH)):
+            nc.scalar.activation(woven(rounded(slice(3 * CH + a, 3 * CH + b))), planar(late[:, 2, :, a:b]), EXP)
+        round_y(vcopy, cols(1))
+        quantise_y(cols(0))
         round_y(vcopy, cols(2))
-        quantise_y(cols(0, 2))
+        quantise_y(cols(1))
         quantise_y(cols(2))
         store_words(cols(0, 3))
-        quantise_y(cols(3))
+        quantise_y(slice(3 * CH, NQ - LAST))
+        quantise_y(slice(NQ - LAST, NQ))
         store_words(cols(3))
         store_scales(nc.scalar, 0)
         store_scales(nc.sync, 1)

from contextlib import ExitStack

import concourse.mybir as mybir

F32 = mybir.dt.float32
BF16 = mybir.dt.bfloat16
I32 = mybir.dt.int32
U32 = mybir.dt.uint32
U16 = mybir.dt.uint16
U8 = mybir.dt.uint8
FP8X4 = mybir.dt.float8_e4m3fn_x4
EXP = mybir.ActivationFunctionType.Exp
SUB = mybir.AluOpType.subtract
ADD = mybir.AluOpType.add
MULT = mybir.AluOpType.mult
EQUAL = mybir.AluOpType.is_equal

P = 128
PACK = 4
N, T, D, NQ = 512, 2048, 512, 512
CH = 128
CHUNKS = NQ // CH
FIRST = 576
LAST = 64
BURST = 256
FLOPS = 2 * N * D * NQ
WIDTH = {F32: 4, U32: 4, BF16: 2, U8: 1}


def woven(dst):
    return dst.rearrange("p (c i) t -> p c t i", i=4)


def planar(src):
    return src.rearrange("p t (c i) -> p c t i", i=4)


def cols(c, end=None):
    return slice(c * CH, (c + 1 if end is None else end) * CH)


def tile_attend_plw_soft_kernel(tc, qT, k_words, k_scales, ls, offs, out_0, out_1, out_2):
    nc = tc.nc
    with ExitStack() as ctx:
        keep = ctx.enter_context(tc.tile_pool(name="keep", bufs=1))
        placed = ctx.enter_context(tc.tile_pool(name="placed", bufs=1))
        psum = ctx.enter_context(tc.psum_pool(name="psum", bufs=1))

        q_rows = qT[0].rearrange("(p j) q -> p j q", j=PACK)
        k_rows = k_words[0].rearrange("p t r -> p (t r)").bitcast(I32)
        y_rows = out_0.rearrange("(p r) q -> p r q", r=PACK)
        y_words = out_1[0].rearrange("p q u -> p (q u)").bitcast(I32)

        spot = {"free": 0}

        def sbuf(shape, dtype, name, over="free", shift=0):
            size = WIDTH[dtype]
            for n in shape[1:]:
                size = size * n
            spot[name] = spot[over] + shift
            if over == "free":
                spot["free"] = spot["free"] + -(-size // BURST) * BURST
            return placed.tile(shape, dtype, name=name, offset=spot[name], align_bytes=BURST)

        vcopy = nc.vector.tensor_copy
        scopy = nc.scalar.copy

        offsets = keep.tile([P, N // 16], U16, name="offsets")
        ls_cols = keep.tile([P, PACK], F32, name="ls_cols")
        pool_words = sbuf([P, T], U32, "pool_words")
        pool_scales = sbuf([P, T], U8, "pool_scales")
        ident = sbuf([P, P], F32, "ident")
        ls_rows = sbuf([P, NQ], F32, "ls_rows")
        k_plane = sbuf([P, N], U8, "k_plane")
        k_codes = sbuf([P, N], U32, "k_codes")
        late = sbuf([P, CHUNKS - 1, PACK, CH], F32, "late")
        y = sbuf([P, PACK, NQ], F32, "y")
        pieces = [(0, 1), (1, 3), (3, 4)]
        q_raw = [sbuf([P, PACK, (b - a) * CH], F32, "q_raw%d" % i) for i, (a, b) in enumerate(pieces[:2])]
        q_raw.append(sbuf([P, PACK, CH], F32, "q_raw2", "y", -1024))
        q_bf = [sbuf([P, CH, PACK], BF16, "q_bf%d" % c) for c in range(CHUNKS)]
        y_bf = sbuf([P, NQ, PACK], BF16, "y_bf")
        y_plane = sbuf([P, NQ], U8, "y_plane")
        q_codes = [sbuf([P, CH], U32, "q_codes%d" % c) for c in range(CHUNKS)]
        q_plane = [sbuf([P, CH], U8, "q_plane%d" % c, "y_plane" if c in (0, 3) else "free") for c in range(CHUNKS)]
        early = sbuf([P, PACK, CH], F32, "early", "q_raw1")
        y_codes = sbuf([P, NQ], U32, "y_codes")
        ls_bank = psum.tile([P, PACK, P], F32, name="ls_bank", tag="turned")
        banks = [
            psum.tile([P, 2, CH], F32, name="bank%d" % u, tag={0: "first", 2 * CHUNKS - 1: "turned"}.get(u, ""))
            for u in range(2 * CHUNKS)
        ]
        last_bank = psum.tile([P, CH], F32, name="last_bank", tag="first")

        def load_scales(queue, j):
            queue.dma_start(pool_scales[j:P:32, :].bitcast(I32), k_scales[0, j:16:4, :].bitcast(I32))

        def load_q(i):
            nc.sync.dma_start(q_raw[i][:], q_rows[:, :, cols(*pieces[i])])

        def round_q(copy, c, a=0, b=CH):
            i = max(i for i, piece in enumerate(pieces) if piece[0] <= c)
            first = (c - pieces[i][0]) * CH
            copy(woven(q_bf[c][:, a:b, :]), planar(q_raw[i][:, :, first + a : first + b]))

        def quantise_q(c):
            nc.vector.quantize_mx(
                out=q_codes[c][:].bitcast(FP8X4),
                scales=q_plane[c][:],
                in_=q_bf[c][:].rearrange("p q j -> p (q j)"),
            )

        def scores(c):
            for r in range(PACK):
                nc.tensor.matmul_mx(
                    out=last_bank[:] if (c, r) == (3, 3) else banks[2 * c + r // 2][:, r % 2, :],
                    lhsT=k_codes[:, r * P : (r + 1) * P].bitcast(FP8X4),
                    lhsT_scale=k_plane[:, r * P : (r + 1) * P],
                    rhs=q_codes[c][:].bitcast(FP8X4),
                    rhs_scale=q_plane[c][:],
                    start=True,
                    stop=True,
                )

        def weights(c, r):
            part = early[:, r : r + 2, :] if c == 0 else late[:, c - 1, r : r + 2, :]
            nc.vector.tensor_tensor(
                part,
                banks[2 * c + r // 2][:],
                ls_rows[:, cols(c)].unsqueeze(1).to_broadcast([P, 2, CH]),
                SUB,
            )
            nc.scalar.activation(y[:, r : r + 2, cols(c)], part, EXP)

        def one_place(r, bank):
            part = late[:, 2, r, :]
            nc.vector.tensor_tensor(part, bank, ls_rows[:, cols(3)], SUB)
            nc.scalar.activation(y[:, r, cols(3)], part, EXP)

        def rounded(span):
            return y_bf[:, span, :]

        def round_early(span):
            nc.gpsimd.tensor_scalar(rounded(span), y[:, :, span].rearrange("p t q -> p q t"), 1.0, 0.0, MULT, ADD)

        def store_weights(span, r0, r1):
            nc.sync.dma_start(y_rows[:, r0:r1, span], y[:, r0:r1, span])

        def round_y(copy, span):
            copy(woven(rounded(span)), planar(y[:, :, span]))

        def quantise_y(span):
            nc.vector.quantize_mx(
                out=y_codes[:, span].bitcast(FP8X4),
                scales=y_plane[:, span],
                in_=rounded(span).rearrange("p q u -> p (q u)"),
            )

        def store_words(span):
            nc.sync.dma_start(y_words[:, span], y_codes[:, span].bitcast(I32))

        def store_scales(queue, j):
            queue.dma_start(out_2[0, j:16:4, :].bitcast(I32), y_plane[j:P:32, :].bitcast(I32))

        def spread_ls():
            ones = keep.tile([P, 32], F32, name="ones")
            column = sbuf([P, 32], F32, "column")
            row = sbuf([P, 32], F32, "row")
            nc.vector.memset(ident[:], 0.0)
            nc.vector.memset(ones[:], 1.0)
            nc.vector.tensor_tensor_scan(column[:], ones[:], ones[:], 0.0, MULT, ADD)
            nc.vector.transpose(row[:], column[:])
            for quad in range(4):
                part = slice(32 * quad, 32 * quad + 32)
                nc.vector.tensor_tensor(ident[part, part], column[part, :], row[part, :], EQUAL)
            for j in range(PACK):
                nc.tensor.transpose(ls_bank[:, j, :], ls_cols[:, j : j + 1].to_broadcast([P, P]), ident[:])
            nc.scalar.copy(ls_rows[:].rearrange("p (n j) -> p n j", j=PACK), ls_bank[:].rearrange("p j n -> p n j"))

        nc.vector.memset(pool_scales[:].bitcast(I32), 0)
        nc.sync.dma_start(pool_words[:, 0:FIRST].bitcast(I32), k_rows[:, 0:FIRST])
        nc.sync.dma_start(offsets[:], offs)
        nc.scalar.dma_start(ls_cols[:], ls[0, 0].rearrange("(p j) -> p j", j=PACK))
        for j in range(4):
            load_scales(nc.scalar if j % 2 else nc.sync, j)
        nc.sync.dma_start(pool_words[:, FIRST:T].bitcast(I32), k_rows[:, FIRST:T])
        for i in range(len(pieces)):
            load_q(i)
        spread_ls()

        vcopy(k_plane[:].rearrange("p (r s) -> p s r", r=PACK), pool_scales[:].indirect(offsets[:]))
        vcopy(k_codes[:].rearrange("p (r s) -> p s r", r=PACK), pool_words[:].indirect(offsets[:]))

        round_q(scopy, 0)
        quantise_q(0)
        scores(0)
        for c in (1, 2):
            round_q(vcopy, c, 0, 80)
            round_q(scopy, c, 80, CH)
        round_q(scopy, 3)
        quantise_q(1)
        scores(1)
        quantise_q(2)
        scores(2)
        weights(0, 0)
        store_weights(cols(0), 0, 2)
        weights(0, 2)
        store_weights(cols(0), 2, 4)
        round_early(cols(0))
        quantise_q(3)
        scores(3)
        weights(1, 0)
        store_weights(cols(1), 0, 2)
        weights(1, 2)
        store_weights(cols(1), 2, 4)
        weights(2, 0)
        weights(2, 2)
        store_weights(cols(2), 0, PACK)
        weights(3, 0)
        one_place(2, banks[7][:, 0, :])
        one_place(3, last_bank[:])
        store_weights(cols(3), 0, PACK)
        for a, b in ((0, CH - LAST), (CH - LAST, CH)):
            nc.scalar.activation(woven(rounded(slice(3 * CH + a, 3 * CH + b))), planar(late[:, 2, :, a:b]), EXP)
        round_y(vcopy, cols(1))
        quantise_y(cols(0))
        round_y(vcopy, cols(2))
        quantise_y(cols(1))
        quantise_y(cols(2))
        store_words(cols(0, 3))
        quantise_y(slice(3 * CH, NQ - LAST))
        quantise_y(slice(NQ - LAST, NQ))
        store_words(cols(3))
        store_scales(nc.scalar, 0)
        store_scales(nc.sync, 1)
        store_scales(nc.scalar, 2)
        store_scales(nc.scalar, 3)
